import numpy as np
import ml_dtypes


def mxq(x, axis, fmt="e4m3"):
    dtype, down = {"e4m3": (ml_dtypes.float8_e4m3fn, 7), "e5m2": (ml_dtypes.float8_e5m2, 14)}[fmt]
    v = np.moveaxis(np.asarray(x, np.float32).astype(ml_dtypes.bfloat16).astype(np.float64), axis, -1)
    blocks = v.reshape(v.shape[:-1] + (-1, 32))
    amax = np.abs(blocks).max(-1, keepdims=True)
    byte = np.maximum(np.where(amax > 0, np.frexp(amax)[1] - 1 + 127, 0) - down, 1)
    scale = np.exp2(byte - 127.0)
    codes = (blocks / scale).astype(np.float32).astype(dtype).astype(np.float64)
    return np.moveaxis((codes * scale).reshape(v.shape), -1, axis)


WIDE = False


def mx_kscale(k):
    if not WIDE:
        return np.ones(k)
    levels = np.array([10, -10, 5, -5, 0])
    if k % 512:
        return np.exp2(np.random.permutation(np.resize(levels, k // 32))).repeat(32)
    a = np.empty((k // 512, 16))
    for p in range(k // 512):
        a[p, :8] = np.random.permutation(np.resize(levels, 8))
        for g in range(8):
            far = levels[np.abs(levels - a[p, g]) >= 10]
            a[p, g + 8] = far[np.random.randint(len(far))]
    return np.exp2(a.ravel()).repeat(32)


def f64(x):
    return np.asarray(x).astype(np.float64)


def striped(idx):
    return np.tile(idx.reshape(-1, 16).T, (8, 1)).astype(np.uint16)


def unstriped(offs):
    return offs[:16].T.reshape(-1).astype(np.int64)


K, T, S, N = 512, 4096, 1024, 512


def setup_inputs():
    n = np.random.standard_normal
    s = mx_kscale(K)[:, None]
    w1, w2 = n((2, K, N)) / np.sqrt(2 * K) / s[None]
    return {
        "xT": (n((K, S)) * s).astype(np.float32),
        "sT": (n((K, T)) * s).astype(np.float32),
        "w1": w1.astype(np.float32),
        "w2": w2.astype(np.float32),
        "offs": striped(np.random.permutation(T)[:S]),
    }


def reference(xT, sT, w1, w2, offs):
    y = mxq(f64(w1), 0, "e4m3").T @ mxq(f64(xT), 0, "e4m3") + mxq(f64(w2), 0, "e4m3").T @ mxq(f64(sT)[:, unstriped(offs)], 0, "e4m3")
    return y

@@ -1,0 +1,132 @@
+from contextlib import ExitStack
+
+import concourse.mybir as mybir
+
+K, T, S, N = 512, 4096, 1024, 512
+FLOPS = 2 * 2 * K * S * N
+
+F32 = mybir.dt.float32
+BF16 = mybir.dt.bfloat16
+U32 = mybir.dt.uint32
+U16 = mybir.dt.uint16
+U8 = mybir.dt.uint8
+FP8X4 = mybir.dt.float8_e4m3fn_x4
+
+P = 128
+PACK = 4
+HALF = S // 2
+M_BLOCKS = N // P
+UNIT = 256
+
+
+def tile_picked_recall_none_e_kernel(tc, xT, sT, w1, w2, offs, out):
+    nc = tc.nc
+    with ExitStack() as ctx:
+        lists = ctx.enter_context(tc.tile_pool(name="lists", bufs=1))
+        keep = ctx.enter_context(tc.tile_pool(name="keep", bufs=1))
+        psum = ctx.enter_context(tc.psum_pool(name="psum", bufs=1))
+
+        offsets = lists.tile([P, S // 16], U16, name="offsets")
+
+        x_rows = xT.rearrange("(p j) c -> p j c", j=PACK)
+        s_rows = sT.rearrange("(p j) t -> p j t", j=PACK)
+        w_raw = {}
+        for i, w in ((2, w2), (1, w1)):
+            w_raw[i] = keep.tile([P, PACK, N], F32, name="w_raw%d" % i)
+            nc.sync.dma_start(out=w_raw[i][:], in_=w.rearrange("(p j) c -> p j c", j=PACK))
+            if i == 2:
+                nc.sync.dma_start(offsets[:], offs)
+        planes = []
+        for j in range(PACK):
+            plane = keep.tile([P, T], F32, name="plane%d" % j)
+            nc.sync.dma_start(out=plane[:], in_=s_rows[:, j, :])
+            planes.append(plane)
+        x_raw = keep.tile([P, PACK, S], F32, name="x_raw")
+        for c0, c1 in ((0, 256), (256, 512), (512, 1024)):
+            nc.sync.dma_start(out=x_raw[:, :, c0:c1], in_=x_rows[:, :, c0:c1])
+
+        def operand(name, width):
+            grouped = keep.tile([P, width, PACK], BF16, name=name + "_grouped", align_bytes=64)
+            codes = keep.tile([P, width], U32, name=name + "_codes", align_bytes=64)
+            scales = keep.tile([P, width], U8, name=name + "_scales", align_bytes=64)
+            return grouped, codes, scales
+
+        def interleave(copy, op, raw, c0, c1):
+            copy(out=op[0][:, c0:c1, :], in_=raw[:, :, c0:c1].rearrange("p j c -> p c j"))
+
+        def quantize(op, c0, c1):
+            nc.vector.quantize_mx(
+                out=op[1][:, c0:c1].bitcast(FP8X4),
+                scales=op[2][:, c0:c1],
+                in_=op[0][:, c0:c1, :].rearrange("p c j -> p (c j)"),
+            )
+
+        def gather(h, j):
+            nc.vector.tensor_copy(
+                out=s_op[0][:, h * HALF : (h + 1) * HALF, j],
+                in_=planes[j][:].indirect(offsets[:, h * HALF // 16 : (h + 1) * HALF // 16]),
+            )
+
+        def mx(acc, w, op, m, c0, start):
+            rows = slice(m * P, (m + 1) * P)
+            cols = slice(c0, c0 + UNIT)
+            nc.tensor.matmul_mx(
+                out=acc[:],
+                lhsT=w[1][:, rows].bitcast(FP8X4),
+                lhsT_scale=w[2][:, rows],
+                rhs=op[1][:, cols].bitcast(FP8X4),
+                rhs_scale=op[2][:, cols],
+                start=start,
+                stop=not start,
+            )
+
+        w_op = {}
+        for i in (2, 1):
+            w_op[i] = operand("w%d" % i, N)
+            interleave(nc.scalar.copy, w_op[i], w_raw[i], 0, N)
+            quantize(w_op[i], 0, N)
+        s_op = operand("s", S)
+        x_op = operand("x", S)
+
+        for j in range(3):
+            gather(0, j)
+            gather(1, j)
+
+        def first(u):
+            accs = [psum.tile([P, UNIT], F32, name="acc%d_%d" % (u, m), tag="bank%d_%d" % (u % 2, m)) for m in range(M_BLOCKS)]
+            for m in range(M_BLOCKS):
+                mx(accs[m], w_op[2], s_op, m, u * UNIT, True)
+            return accs
+
+        def second(u, accs, copies):
+            for m in range(M_BLOCKS):
+                mx(accs[m], w_op[1], x_op, m, u * UNIT, False)
+                result = keep.tile([P, UNIT], F32, name="result%d_%d" % (u, m))
+                copies[m](out=result[:], in_=accs[m][:])
+                nc.sync.dma_start(out=out[m * P : (m + 1) * P, u * UNIT : (u + 1) * UNIT], in_=result[:])
+
+        v, s = nc.vector.tensor_copy, nc.scalar.copy
+
+        interleave(s, x_op, x_raw, 0, 128)
+        interleave(v, x_op, x_raw, 128, 256)
+        gather(0, 3)
+        quantize(s_op, 0, 256)
+        quantize(x_op, 0, 256)
+        accs = first(0)
+        second(0, accs, [s, s, s, s])
+        interleave(s, x_op, x_raw, 256, 512)
+        gather(1, 3)
+        quantize(s_op, 256, 512)
+        quantize(x_op, 256, 512)
+        accs = first(1)
+        interleave(v, x_op, x_raw, 512, 768)
+        second(1, accs, [s, s, s, s])
+        quantize(s_op, 512, 768)
+        quantize(x_op, 512, 768)
+        accs = first(2)
+        second(2, accs, [s, s, s, v])
+        interleave(v, x_op, x_raw, 768, 1024)
+        quantize(s_op, 768, 1024)
+        quantize(x_op, 768, 1024)
+        accs = first(3)
+        second(3, accs, [v, s, v, s])

@@ -28,22 +28,23 @@ def tile_picked_recall_none_e_kernel(tc, xT, sT, w1, w2, offs, out):
 
         offsets = lists.tile([P, S // 16], U16, name="offsets")
 
-        x_rows = xT.rearrange("(p j) c -> p j c", j=PACK)
         s_rows = sT.rearrange("(p j) t -> p j t", j=PACK)
-        w_raw = {}
-        for i, w in ((2, w2), (1, w1)):
-            w_raw[i] = keep.tile([P, PACK, N], F32, name="w_raw%d" % i)
-            nc.sync.dma_start(out=w_raw[i][:], in_=w.rearrange("(p j) c -> p j c", j=PACK))
-            if i == 2:
-                nc.sync.dma_start(offsets[:], offs)
         planes = []
         for j in range(PACK):
             plane = keep.tile([P, T], F32, name="plane%d" % j)
             nc.sync.dma_start(out=plane[:], in_=s_rows[:, j, :])
             planes.append(plane)
-        x_raw = keep.tile([P, PACK, S], F32, name="x_raw")
-        for c0, c1 in ((0, 256), (256, 512), (512, 1024)):
-            nc.sync.dma_start(out=x_raw[:, :, c0:c1], in_=x_rows[:, :, c0:c1])
+            if j == 0:
+                nc.sync.dma_start(offsets[:], offs)
+
+        def load(name, src, c0, c1):
+            raw = keep.tile([P, PACK, c1 - c0], F32, name=name + "_raw")
+            nc.sync.dma_start(out=raw[:], in_=src.rearrange("(p j) c -> p j c", j=PACK)[:, :, c0:c1])
+            return raw
+
+        w2_raw = [load("w2_%d" % h, w2, h * UNIT, (h + 1) * UNIT) for h in range(2)]
+        w1_raw = [load("w1_%d" % h, w1, h * UNIT, (h + 1) * UNIT) for h in range(2)]
+        x_raw = [load("x_%d" % u, xT, u * UNIT, (u + 1) * UNIT) for u in range(4)]
 
         def operand(name, width):
             grouped = keep.tile([P, width, PACK], BF16, name=name + "_grouped", align_bytes=64)
@@ -51,82 +52,85 @@ def tile_picked_recall_none_e_kernel(tc, xT, sT, w1, w2, offs, out):
             scales = keep.tile([P, width], U8, name=name + "_scales", align_bytes=64)
             return grouped, codes, scales
 
-        def interleave(copy, op, raw, c0, c1):
-            copy(out=op[0][:, c0:c1, :], in_=raw[:, :, c0:c1].rearrange("p j c -> p c j"))
+        def interleave(copy, op, raw):
+            copy(out=op[0][:], in_=raw[:].rearrange("p j c -> p c j"))
 
-        def quantize(op, c0, c1):
+        def quantize(op):
             nc.vector.quantize_mx(
-                out=op[1][:, c0:c1].bitcast(FP8X4),
-                scales=op[2][:, c0:c1],
-                in_=op[0][:, c0:c1, :].rearrange("p c j -> p (c j)"),
+                out=op[1][:].bitcast(FP8X4),
+                scales=op[2][:],
+                in_=op[0][:].rearrange("p c j -> p (c j)"),
             )
+
+        s_op = [operand("s%d" % h, HALF) for h in range(2)]
+        w2_op = [operand("w2_%d" % h, UNIT) for h in range(2)]
+        w1_op = [operand("w1_%d" % h, UNIT) for h in range(2)]
+        x_op = [operand("x%d" % u, UNIT) for u in range(4)]
 
         def gather(h, j):
             nc.vector.tensor_copy(
-                out=s_op[0][:, h * HALF : (h + 1) * HALF, j],
+                out=s_op[h][0][:, :, j],
                 in_=planes[j][:].indirect(offsets[:, h * HALF // 16 : (h + 1) * HALF // 16]),
             )
 
-        def mx(acc, w, op, m, c0, start):
-            rows = slice(m * P, (m + 1) * P)
+        def mx(acc, w, m, op, c0, start):
+            rows = slice((m % 2) * P, (m % 2 + 1) * P)
             cols = slice(c0, c0 + UNIT)
             nc.tensor.matmul_mx(
                 out=acc[:],
-                lhsT=w[1][:, rows].bitcast(FP8X4),
-                lhsT_scale=w[2][:, rows],
+                lhsT=w[m // 2][1][:, rows].bitcast(FP8X4),
+                lhsT_scale=w[m // 2][2][:, rows],
                 rhs=op[1][:, cols].bitcast(FP8X4),
                 rhs_scale=op[2][:, cols],
                 start=start,
                 stop=not start,
             )
 
-        w_op = {}
-        for i in (2, 1):
-            w_op[i] = operand("w%d" % i, N)
-            interleave(nc.scalar.copy, w_op[i], w_raw[i], 0, N)
-            quantize(w_op[i], 0, N)
-        s_op = operand("s", S)
-        x_op = operand("x", S)
-
-        for j in range(3):
-            gather(0, j)
-            gather(1, j)
+        out_rows = out.rearrange("(m p) c -> p m c", p=P)
 
         def first(u):
             accs = [psum.tile([P, UNIT], F32, name="acc%d_%d" % (u, m), tag="bank%d_%d" % (u % 2, m)) for m in range(M_BLOCKS)]
             for m in range(M_BLOCKS):
-                mx(accs[m], w_op[2], s_op, m, u * UNIT, True)
+                mx(accs[m], w2_op, m, s_op[u // 2], (u % 2) * UNIT, True)
             return accs
 
         def second(u, accs, copies):
-            for m in range(M_BLOCKS):
-                mx(accs[m], w_op[1], x_op, m, u * UNIT, False)
-                result = keep.tile([P, UNIT], F32, name="result%d_%d" % (u, m))
-                copies[m](out=result[:], in_=accs[m][:])
-                nc.sync.dma_start(out=out[m * P : (m + 1) * P, u * UNIT : (u + 1) * UNIT], in_=result[:])
+            for pair in range(2):
+                result = keep.tile([P, 2, UNIT], F32, name="result%d_%d" % (u, pair))
+                for i in range(2):
+                    m = 2 * pair + i
+                    mx(accs[m], w1_op, m, x_op[u], 0, False)
+                    copies[m](out=result[:, i, :], in_=accs[m][:])
+                nc.sync.dma_start(out=out_rows[:, 2 * pair : 2 * pair + 2, u * UNIT : (u + 1) * UNIT], in_=result[:])
 
         v, s = nc.vector.tensor_copy, nc.scalar.copy
 
-        interleave(s, x_op, x_raw, 0, 128)
-        interleave(v, x_op, x_raw, 128, 256)
-        gather(0, 3)
-        quantize(s_op, 0, 256)
-        quantize(x_op, 0, 256)
-        accs = first(0)
-        second(0, accs, [s, s, s, s])
-        interleave(s, x_op, x_raw, 256, 512)
-        gather(1, 3)
-        quantize(s_op, 256, 512)
-        quantize(x_op, 256, 512)
-        accs = first(1)
-        interleave(v, x_op, x_raw, 512, 768)
-        second(1, accs, [s, s, s, s])
-        quantize(s_op, 512, 768)
-        quantize(x_op, 512, 768)
-        accs = first(2)
-        second(2, accs, [s, s, s, v])
-        interleave(v, x_op, x_raw, 768, 1024)
-        quantize(s_op, 768, 1024)
-        quantize(x_op, 768, 1024)
-        accs = first(3)
-        second(3, accs, [v, s, v, s])
+        for j in range(PACK):
+            gather(0, j)
+            gather(1, j)
+        interleave(s, w2_op[0], w2_raw[0])
+        interleave(s, w2_op[1], w2_raw[1])
+        interleave(s, w1_op[0], w1_raw[0])
+        quantize(w2_op[0])
+        quantize(s_op[0])
+        quantize(w2_op[1])
+        accs0 = first(0)
+        accs1 = first(1)
+        interleave(v, w1_op[1], w1_raw[1])
+        interleave(s, x_op[0], x_raw[0])
+        quantize(w1_op[0])
+        quantize(w1_op[1])
+        quantize(s_op[1])
+        quantize(x_op[0])
+        interleave(v, x_op[1], x_raw[1])
+        second(0, accs0, [s, s, s, s])
+        quantize(x_op[1])
+        interleave(v, x_op[2], x_raw[2])
+        second(1, accs1, [s, s, s, s])
+        accs2 = first(2)
+        quantize(x_op[2])
+        interleave(v, x_op[3], x_raw[3])
+        second(2, accs2, [s, s, s, s])
+        accs3 = first(3)
+        quantize(x_op[3])
+        second(3, accs3, [v, s, v, s])

@@ -53,7 +53,10 @@ def tile_picked_recall_none_e_kernel(tc, xT, sT, w1, w2, offs, out):
             return grouped, codes, scales
 
         def interleave(copy, op, raw):
-            copy(out=op[0][:], in_=raw[:].rearrange("p j c -> p c j"))
+            copy(
+                out=op[0][:].rearrange("p (c i) j -> p c j i", i=4),
+                in_=raw[:].rearrange("p j (c i) -> p c j i", i=4),
+            )
 
         def quantize(op):
             nc.vector.quantize_mx(

@@ -76,6 +76,15 @@ def tile_picked_recall_none_e_kernel(tc, xT, sT, w1, w2, offs, out):
                 in_=planes[j][:].indirect(offsets[:, h * HALF // 16 : (h + 1) * HALF // 16]),
             )
 
+        def gather_by_scalar(h, j):
+            picked = keep.tile([P, HALF], BF16, name="picked%d" % j)
+            nc.scalar.activation(
+                picked[:],
+                planes[j][:].indirect(offsets[:, h * HALF // 16 : (h + 1) * HALF // 16]),
+                mybir.ActivationFunctionType.Copy,
+            )
+            nc.vector.tensor_copy(out=s_op[h][0][:, :, j], in_=picked[:])
+
         def mx(acc, w, m, op, c0, start):
             rows = slice((m % 2) * P, (m % 2 + 1) * P)
             cols = slice(c0, c0 + UNIT)
@@ -110,7 +119,7 @@ def tile_picked_recall_none_e_kernel(tc, xT, sT, w1, w2, offs, out):
 
         for j in range(PACK):
             gather(0, j)
-            gather(1, j)
+            gather_by_scalar(1, j)
         interleave(s, w2_op[0], w2_raw[0])
         interleave(s, w2_op[1], w2_raw[1])
         interleave(s, w1_op[0], w1_raw[0])

@@ -15,7 +15,6 @@ FP8X4 = mybir.dt.float8_e4m3fn_x4
 P = 128
 PACK = 4
 HALF = S // 2
-M_BLOCKS = N // P
 UNIT = 256
 
 
@@ -25,6 +24,7 @@ def tile_picked_recall_none_e_kernel(tc, xT, sT, w1, w2, offs, out):
         lists = ctx.enter_context(tc.tile_pool(name="lists", bufs=1))
         keep = ctx.enter_context(tc.tile_pool(name="keep", bufs=1))
         psum = ctx.enter_context(tc.psum_pool(name="psum", bufs=1))
+        v, s = nc.vector.tensor_copy, nc.scalar.copy
 
         offsets = lists.tile([P, S // 16], U16, name="offsets")
 
@@ -38,111 +38,133 @@ def tile_picked_recall_none_e_kernel(tc, xT, sT, w1, w2, offs, out):
                 nc.sync.dma_start(offsets[:], offs)
 
         def load(name, src, c0, c1):
-            raw = keep.tile([P, PACK, c1 - c0], F32, name=name + "_raw")
+            raw = keep.tile([P, PACK, c1 - c0], F32, name=name + "_raw", tag=name + "_raw", align_bytes=64)
             nc.sync.dma_start(out=raw[:], in_=src.rearrange("(p j) c -> p j c", j=PACK)[:, :, c0:c1])
             return raw
 
-        w2_raw = [load("w2_%d" % h, w2, h * UNIT, (h + 1) * UNIT) for h in range(2)]
-        w1_raw = [load("w1_%d" % h, w1, h * UNIT, (h + 1) * UNIT) for h in range(2)]
-        x_raw = [load("x_%d" % u, xT, u * UNIT, (u + 1) * UNIT) for u in range(4)]
+        def operand(name, cuts, tags={}):
+            return [
+                (
+                    c0,
+                    c1,
+                    keep.tile([P, c1 - c0], U32, name="%s_codes%d" % (name, c0), tag=tags.get(c0, "%s_codes%d" % (name, c0)), align_bytes=64),
+                    keep.tile([P, c1 - c0], U8, name="%s_scales%d" % (name, c0), align_bytes=64),
+                )
+                for c0, c1 in zip(cuts, cuts[1:])
+            ]
 
-        def operand(name, width):
-            grouped = keep.tile([P, width, PACK], BF16, name=name + "_grouped", align_bytes=64)
-            codes = keep.tile([P, width], U32, name=name + "_codes", align_bytes=64)
-            scales = keep.tile([P, width], U8, name=name + "_scales", align_bytes=64)
-            return grouped, codes, scales
+        def columns(op, c0, c1):
+            first, last, codes, scales = [piece for piece in op if piece[0] <= c0 and c1 <= piece[1]][0]
+            return codes[:, c0 - first : c1 - first].bitcast(FP8X4), scales[:, c0 - first : c1 - first]
 
-        def interleave(copy, op, raw):
+        def interleave(copy, name, raw, c0, c1, tag=None):
+            grouped = keep.tile([P, c1 - c0, PACK], BF16, name=name + "_grouped", tag=tag or name, align_bytes=64)
             copy(
-                out=op[0][:].rearrange("p (c i) j -> p c j i", i=4),
-                in_=raw[:].rearrange("p j (c i) -> p c j i", i=4),
+                out=grouped[:].rearrange("p (c i) j -> p c j i", i=4),
+                in_=raw[:, :, c0:c1].rearrange("p j (c i) -> p c j i", i=4),
             )
+            return grouped[:]
 
-        def quantize(op):
-            nc.vector.quantize_mx(
-                out=op[1][:].bitcast(FP8X4),
-                scales=op[2][:],
-                in_=op[0][:].rearrange("p c j -> p (c j)"),
-            )
+        def quantize(op, c0, grouped):
+            codes, scales = columns(op, c0, c0 + grouped.shape[1])
+            nc.vector.quantize_mx(out=codes, scales=scales, in_=grouped.rearrange("p c j -> p (c j)"))
 
-        s_op = [operand("s%d" % h, HALF) for h in range(2)]
-        w2_op = [operand("w2_%d" % h, UNIT) for h in range(2)]
-        w1_op = [operand("w1_%d" % h, UNIT) for h in range(2)]
-        x_op = [operand("x%d" % u, UNIT) for u in range(4)]
-
-        def gather(h, j):
-            nc.vector.tensor_copy(
-                out=s_op[h][0][:, :, j],
-                in_=planes[j][:].indirect(offsets[:, h * HALF // 16 : (h + 1) * HALF // 16]),
-            )
-
-        def gather_by_scalar(h, j):
-            picked = keep.tile([P, HALF], BF16, name="picked%d" % j)
-            nc.scalar.activation(
-                picked[:],
-                planes[j][:].indirect(offsets[:, h * HALF // 16 : (h + 1) * HALF // 16]),
-                mybir.ActivationFunctionType.Copy,
-            )
-            nc.vector.tensor_copy(out=s_op[h][0][:, :, j], in_=picked[:])
-
-        def mx(acc, w, m, op, c0, start):
-            rows = slice((m % 2) * P, (m % 2 + 1) * P)
-            cols = slice(c0, c0 + UNIT)
+        def mx(acc, w, m, op, c0, c1, start, stop):
+            w_codes, w_scales = columns(w, m * P, (m + 1) * P)
+            codes, scales = columns(op, c0, c1)
             nc.tensor.matmul_mx(
-                out=acc[:],
-                lhsT=w[m // 2][1][:, rows].bitcast(FP8X4),
-                lhsT_scale=w[m // 2][2][:, rows],
-                rhs=op[1][:, cols].bitcast(FP8X4),
-                rhs_scale=op[2][:, cols],
-                start=start,
-                stop=not start,
+                out=acc, lhsT=w_codes, lhsT_scale=w_scales, rhs=codes, rhs_scale=scales, start=start, stop=stop
             )
 
         out_rows = out.rearrange("(m p) c -> p m c", p=P)
+        s_grouped = [keep.tile([P, HALF, PACK], BF16, name="s_grouped%d" % h, align_bytes=64) for h in range(2)]
 
-        def first(u):
-            accs = [psum.tile([P, UNIT], F32, name="acc%d_%d" % (u, m), tag="bank%d_%d" % (u % 2, m)) for m in range(M_BLOCKS)]
-            for m in range(M_BLOCKS):
-                mx(accs[m], w2_op, m, s_op[u // 2], (u % 2) * UNIT, True)
-            return accs
+        def gathers():
+            for j in range(PACK):
+                nc.vector.tensor_copy(out=s_grouped[0][:, :, j], in_=planes[j][:].indirect(offsets[:, : HALF // 16]))
+                picked = keep.tile([P, HALF], BF16, name="picked%d" % j)
+                nc.scalar.activation(
+                    picked[:], planes[j][:].indirect(offsets[:, HALF // 16 :]), mybir.ActivationFunctionType.Copy
+                )
+                nc.vector.tensor_copy(out=s_grouped[1][:, :, j], in_=picked[:])
 
-        def second(u, accs, copies):
-            for pair in range(2):
-                result = keep.tile([P, 2, UNIT], F32, name="result%d_%d" % (u, pair))
+
+        def bank(name, b):
+            return psum.tile([P, 2 * UNIT], F32, name=name, tag="bank%d" % b)
+
+        s_op = operand("s", [0, HALF])
+        x_op = operand("x", [0, UNIT, HALF, HALF + UNIT, S])
+        w1_op = operand("w1", [0, UNIT, N])
+        w2_op = operand("w2", [0, UNIT, N])
+
+        w2a, w2b = load("w2a", w2, 0, UNIT), load("w2b", w2, UNIT, N)
+        w1a = load("w1a", w1, 0, UNIT)
+        w1b = load("w1b", w1, UNIT, N)
+        x_raw = [load("x%d" % u, xT, u * UNIT, (u + 1) * UNIT) for u in range(4)]
+
+        def pair_pass(acc, w, op, u, m, opening):
+            part = acc[:, (m % 2) * UNIT : (m % 2 + 1) * UNIT]
+            mx(part, w, m, op, u * UNIT, (u + 1) * UNIT, opening and m % 2 == 0, not opening and m % 2 == 1)
+
+        def close_pair(acc, u, h):
+            for m in (2 * h, 2 * h + 1):
+                pair_pass(acc, w1_op, x_op, u, m, False)
+            result = keep.tile([P, 2, UNIT], F32, name="early%d_%d" % (u, h))
+            s(out=result[:].rearrange("p m c -> p (m c)"), in_=acc[:])
+            nc.sync.dma_start(out=out_rows[:, 2 * h : 2 * h + 2, u * UNIT : (u + 1) * UNIT], in_=result[:])
+            return result
+
+        def open_one(u, m, b):
+            acc = bank("one%d_%d" % (u, m), b)
+            mx(acc[:, :UNIT], w2_op, m, s_op, u * UNIT, (u + 1) * UNIT, True, False)
+            return acc
+
+        def close_unit(accs, u, copies):
+            for h in range(2):
+                result = keep.tile([P, 2, UNIT], F32, name="late%d_%d" % (u, h))
                 for i in range(2):
-                    m = 2 * pair + i
-                    mx(accs[m], w1_op, m, x_op[u], 0, False)
-                    copies[m](out=result[:, i, :], in_=accs[m][:])
-                nc.sync.dma_start(out=out_rows[:, 2 * pair : 2 * pair + 2, u * UNIT : (u + 1) * UNIT], in_=result[:])
+                    m = 2 * h + i
+                    mx(accs[m][:, :UNIT], w1_op, m, x_op, u * UNIT, (u + 1) * UNIT, False, True)
+                    copies[m](out=result[:, i, :], in_=accs[m][:, :UNIT])
+                nc.sync.dma_start(out=out_rows[:, 2 * h : 2 * h + 2, u * UNIT : (u + 1) * UNIT], in_=result[:])
 
-        v, s = nc.vector.tensor_copy, nc.scalar.copy
+        def halves(u, copies):
+            return [interleave(copies[i], "x%d_%d" % (u, i), x_raw[u], i * P, (i + 1) * P) for i in range(2)]
 
-        for j in range(PACK):
-            gather(0, j)
-            gather_by_scalar(1, j)
-        interleave(s, w2_op[0], w2_raw[0])
-        interleave(s, w2_op[1], w2_raw[1])
-        interleave(s, w1_op[0], w1_raw[0])
-        quantize(w2_op[0])
-        quantize(s_op[0])
-        quantize(w2_op[1])
-        accs0 = first(0)
-        accs1 = first(1)
-        interleave(v, w1_op[1], w1_raw[1])
-        interleave(s, x_op[0], x_raw[0])
-        quantize(w1_op[0])
-        quantize(w1_op[1])
-        quantize(s_op[1])
-        quantize(x_op[0])
-        interleave(v, x_op[1], x_raw[1])
-        second(0, accs0, [s, s, s, s])
-        quantize(x_op[1])
-        interleave(v, x_op[2], x_raw[2])
-        second(1, accs1, [s, s, s, s])
-        accs2 = first(2)
-        quantize(x_op[2])
-        interleave(v, x_op[3], x_raw[3])
-        second(2, accs2, [s, s, s, s])
-        accs3 = first(3)
-        quantize(x_op[3])
-        second(3, accs3, [v, s, v, s])
+        def quantize_halves(u, grouped):
+            for i in range(2):
+                quantize(x_op, u * UNIT + i * P, grouped[i])
+
+        gathers()
+        g_w2a = interleave(s, "w2a", w2a, 0, UNIT)
+        g_w2b = interleave(s, "w2b", w2b, 0, UNIT)
+        g_w1a = interleave(s, "w1a", w1a, 0, UNIT)
+        quantize(s_op, 0, s_grouped[0][:])
+        quantize(w2_op, 0, g_w2a)
+        quantize(w2_op, UNIT, g_w2b)
+        s_op = s_op + operand("s", [HALF, S], {HALF: "w2a_raw"})
+        quantize(s_op, HALF, s_grouped[1][:])
+        pairs = {(u, h): bank("pair%d_%d" % (u, h), 2 * u + h) for u in range(3) for h in range(2)}
+        for u, h in [(0, 0), (1, 0), (0, 1), (1, 1), (2, 0), (2, 1)]:
+            for m in (2 * h, 2 * h + 1):
+                pair_pass(pairs[u, h], w2_op, s_op, u, m, True)
+        last = [open_one(3, m, 6 + m) for m in range(2)]
+        g_w1b = interleave(v, "w1b", w1b, 0, UNIT)
+        quantize(w1_op, 0, g_w1a)
+        g_x0 = halves(0, [v, s])
+        quantize(w1_op, UNIT, g_w1b)
+        quantize_halves(0, g_x0)
+        g_x1 = halves(1, [v, s])
+        close_pair(pairs[0, 0], 0, 0)
+        close_pair(pairs[0, 1], 0, 1)
+        quantize_halves(1, g_x1)
+        g_x2 = halves(2, [v, v])
+        close_pair(pairs[1, 0], 1, 0)
+        close_pair(pairs[1, 1], 1, 1)
+        last = last + [open_one(3, m, m - 2) for m in (2, 3)]
+        quantize_halves(2, g_x2)
+        g_x3 = halves(3, [v, v])
+        close_pair(pairs[2, 0], 2, 0)
+        close_pair(pairs[2, 1], 2, 1)
+        quantize_halves(3, g_x3)
+        close_unit(last, 3, [v, s, v, s])

@@ -107,8 +107,15 @@ def tile_picked_recall_none_e_kernel(tc, xT, sT, w1, w2, offs, out):
             mx(part, w, m, op, u * UNIT, (u + 1) * UNIT, opening and m % 2 == 0, not opening and m % 2 == 1)
 
         def close_pair(acc, u, h):
-            for m in (2 * h, 2 * h + 1):
-                pair_pass(acc, w1_op, x_op, u, m, False)
+            if h == 0:
+                for i in range(2):
+                    for m in range(2):
+                        c0 = u * UNIT + i * P
+                        part = acc[:, m * UNIT + i * P : m * UNIT + (i + 1) * P]
+                        mx(part, w1_op, m, x_op, c0, c0 + P, False, (i, m) == (1, 1))
+            else:
+                for m in (2, 3):
+                    pair_pass(acc, w1_op, x_op, u, m, False)
             result = keep.tile([P, 2, UNIT], F32, name="early%d_%d" % (u, h))
             s(out=result[:].rearrange("p m c -> p (m c)"), in_=acc[:])
             nc.sync.dma_start(out=out_rows[:, 2 * h : 2 * h + 2, u * UNIT : (u + 1) * UNIT], in_=result[:])
@@ -154,10 +161,11 @@ def tile_picked_recall_none_e_kernel(tc, xT, sT, w1, w2, offs, out):
         g_x0 = halves(0, [v, s])
         quantize(w1_op, UNIT, g_w1b)
         quantize_halves(0, g_x0)
-        g_x1 = halves(1, [v, s])
+        g_x1 = [interleave(copy, "x1_%d" % c0, x_raw[1], c0, c1) for copy, c0, c1 in ((v, 0, 128), (v, 128, 192), (s, 192, 256))]
         close_pair(pairs[0, 0], 0, 0)
         close_pair(pairs[0, 1], 0, 1)
-        quantize_halves(1, g_x1)
+        for c0, grouped in zip((0, 128, 192), g_x1):
+            quantize(x_op, UNIT + c0, grouped)
         g_x2 = halves(2, [v, v])
         close_pair(pairs[1, 0], 1, 0)
         close_pair(pairs[1, 1], 1, 1)

@@ -94,19 +94,21 @@ def tile_picked_recall_none_e_kernel(tc, xT, sT, w1, w2, offs, out):
 
         s_op = operand("s", [0, HALF])
         x_op = operand("x", [0, UNIT, HALF, HALF + UNIT, S])
-        w1_op = operand("w1", [0, UNIT, N])
+        w1_op = operand("w1", [0, UNIT, UNIT + P, N])
         w2_op = operand("w2", [0, UNIT, N])
 
-        w2a, w2b = load("w2a", w2, 0, UNIT), load("w2b", w2, UNIT, N)
+        w2a = load("w2a", w2, 0, UNIT)
         w1a = load("w1a", w1, 0, UNIT)
+        x_raw = [load("x0", xT, 0, UNIT)]
+        w2b = load("w2b", w2, UNIT, N)
         w1b = load("w1b", w1, UNIT, N)
-        x_raw = [load("x%d" % u, xT, u * UNIT, (u + 1) * UNIT) for u in range(4)]
+        x_raw = x_raw + [load("x%d" % u, xT, u * UNIT, (u + 1) * UNIT) for u in range(1, 4)]
 
         def pair_pass(acc, w, op, u, m, opening):
             part = acc[:, (m % 2) * UNIT : (m % 2 + 1) * UNIT]
             mx(part, w, m, op, u * UNIT, (u + 1) * UNIT, opening and m % 2 == 0, not opening and m % 2 == 1)
 
-        def close_pair(acc, u, h):
+        def close_pair(acc, u, h, tag=None, copy=s):
             if h == 0:
                 for i in range(2):
                     for m in range(2):
@@ -116,8 +118,8 @@ def tile_picked_recall_none_e_kernel(tc, xT, sT, w1, w2, offs, out):
             else:
                 for m in (2, 3):
                     pair_pass(acc, w1_op, x_op, u, m, False)
-            result = keep.tile([P, 2, UNIT], F32, name="early%d_%d" % (u, h))
-            s(out=result[:].rearrange("p m c -> p (m c)"), in_=acc[:])
+            result = keep.tile([P, 2, UNIT], F32, name="early%d_%d" % (u, h), tag=tag or "early%d_%d" % (u, h), align_bytes=64)
+            copy(out=result[:].rearrange("p m c -> p (m c)"), in_=acc[:])
             nc.sync.dma_start(out=out_rows[:, 2 * h : 2 * h + 2, u * UNIT : (u + 1) * UNIT], in_=result[:])
             return result
 
@@ -126,14 +128,15 @@ def tile_picked_recall_none_e_kernel(tc, xT, sT, w1, w2, offs, out):
             mx(acc[:, :UNIT], w2_op, m, s_op, u * UNIT, (u + 1) * UNIT, True, False)
             return acc
 
-        def close_unit(accs, u, copies):
-            for h in range(2):
-                result = keep.tile([P, 2, UNIT], F32, name="late%d_%d" % (u, h))
-                for i in range(2):
-                    m = 2 * h + i
-                    mx(accs[m][:, :UNIT], w1_op, m, x_op, u * UNIT, (u + 1) * UNIT, False, True)
-                    copies[m](out=result[:, i, :], in_=accs[m][:, :UNIT])
-                nc.sync.dma_start(out=out_rows[:, 2 * h : 2 * h + 2, u * UNIT : (u + 1) * UNIT], in_=result[:])
+        def close_blocks(accs, u, copies):
+            result = keep.tile([P, 2, UNIT], F32, name="late%d" % u)
+            for i in range(2):
+                for m in range(2):
+                    c0 = u * UNIT + i * P
+                    mx(accs[m][:, i * P : (i + 1) * P], w1_op, m, x_op, c0, c0 + P, False, i == 1)
+            for m in range(2):
+                copies[m](out=result[:, m, :], in_=accs[m][:, :UNIT])
+            nc.sync.dma_start(out=out_rows[:, :2, u * UNIT : (u + 1) * UNIT], in_=result[:])
 
         def halves(u, copies):
             return [interleave(copies[i], "x%d_%d" % (u, i), x_raw[u], i * P, (i + 1) * P) for i in range(2)]
@@ -144,35 +147,49 @@ def tile_picked_recall_none_e_kernel(tc, xT, sT, w1, w2, offs, out):
 
         gathers()
         g_w2a = interleave(s, "w2a", w2a, 0, UNIT)
-        g_w2b = interleave(s, "w2b", w2b, 0, UNIT)
         g_w1a = interleave(s, "w1a", w1a, 0, UNIT)
         quantize(s_op, 0, s_grouped[0][:])
         quantize(w2_op, 0, g_w2a)
-        quantize(w2_op, UNIT, g_w2b)
         s_op = s_op + operand("s", [HALF, S], {HALF: "w2a_raw"})
         quantize(s_op, HALF, s_grouped[1][:])
-        pairs = {(u, h): bank("pair%d_%d" % (u, h), 2 * u + h) for u in range(3) for h in range(2)}
-        for u, h in [(0, 0), (1, 0), (0, 1), (1, 1), (2, 0), (2, 1)]:
+        def open_pair(u, h):
             for m in (2 * h, 2 * h + 1):
                 pair_pass(pairs[u, h], w2_op, s_op, u, m, True)
+
+        pairs = {(u, h): bank("pair%d_%d" % (u, h), 2 * u + h) for u in range(3) for h in range(2)}
+        def high_half(name, raw):
+            return [interleave(copy, "%s_%d" % (name, i), raw, i * P, (i + 1) * P) for i, copy in enumerate((v, s))]
+
+        def quantize_high(op, grouped):
+            for i in range(2):
+                quantize(op, UNIT + i * P, grouped[i])
+
+        for u in range(3):
+            open_pair(u, 0)
         last = [open_one(3, m, 6 + m) for m in range(2)]
-        g_w1b = interleave(v, "w1b", w1b, 0, UNIT)
-        quantize(w1_op, 0, g_w1a)
         g_x0 = halves(0, [v, s])
-        quantize(w1_op, UNIT, g_w1b)
+        quantize(w1_op, 0, g_w1a)
         quantize_halves(0, g_x0)
-        g_x1 = [interleave(copy, "x1_%d" % c0, x_raw[1], c0, c1) for copy, c0, c1 in ((v, 0, 128), (v, 128, 192), (s, 192, 256))]
-        close_pair(pairs[0, 0], 0, 0)
+        g_w2b = interleave(s, "w2b", w2b, 0, UNIT)
+        g_w1b = high_half("w1b", w1b)
+        quantize(w2_op, UNIT, g_w2b)
+        close_pair(pairs[0, 0], 0, 0, "w1b_raw")
+        open_pair(0, 1)
+        quantize_high(w1_op, g_w1b)
+        g_x1 = halves(1, [v, v])
         close_pair(pairs[0, 1], 0, 1)
-        for c0, grouped in zip((0, 128, 192), g_x1):
-            quantize(x_op, UNIT + c0, grouped)
+        for u in (1, 2):
+            open_pair(u, 1)
+        quantize_halves(1, g_x1)
         g_x2 = halves(2, [v, v])
         close_pair(pairs[1, 0], 1, 0)
         close_pair(pairs[1, 1], 1, 1)
-        last = last + [open_one(3, m, m - 2) for m in (2, 3)]
+        pairs[3, 1] = bank("pair3_1", 0)
+        open_pair(3, 1)
         quantize_halves(2, g_x2)
         g_x3 = halves(3, [v, v])
         close_pair(pairs[2, 0], 2, 0)
         close_pair(pairs[2, 1], 2, 1)
         quantize_halves(3, g_x3)
-        close_unit(last, 3, [v, s, v, s])
+        close_blocks(last, 3, [v, s])
+        close_pair(pairs[3, 1], 3, 1, copy=v)

@@ -16,6 +16,10 @@ P = 128
 PACK = 4
 HALF = S // 2
 UNIT = 256
+LINE = 4
+SCALAR_SHARE = 192
+LOW, HIGH = 0, 1
+LAST = S // UNIT - 1
 
 
 def tile_picked_recall_none_e_kernel(tc, xT, sT, w1, w2, offs, out):
@@ -24,16 +28,16 @@ def tile_picked_recall_none_e_kernel(tc, xT, sT, w1, w2, offs, out):
         lists = ctx.enter_context(tc.tile_pool(name="lists", bufs=1))
         keep = ctx.enter_context(tc.tile_pool(name="keep", bufs=1))
         psum = ctx.enter_context(tc.psum_pool(name="psum", bufs=1))
-        v, s = nc.vector.tensor_copy, nc.scalar.copy
+        on_vector, on_scalar = nc.vector.tensor_copy, nc.scalar.copy
 
         offsets = lists.tile([P, S // 16], U16, name="offsets")
 
         s_rows = sT.rearrange("(p j) t -> p j t", j=PACK)
-        planes = []
+        s_slots = []
         for j in range(PACK):
-            plane = keep.tile([P, T], F32, name="plane%d" % j)
-            nc.sync.dma_start(out=plane[:], in_=s_rows[:, j, :])
-            planes.append(plane)
+            slot = keep.tile([P, T], F32, name="plane%d" % j)
+            nc.sync.dma_start(out=slot[:], in_=s_rows[:, j, :])
+            s_slots.append(slot)
             if j == 0:
                 nc.sync.dma_start(offsets[:], offs)
 
@@ -42,154 +46,162 @@ def tile_picked_recall_none_e_kernel(tc, xT, sT, w1, w2, offs, out):
             nc.sync.dma_start(out=raw[:], in_=src.rearrange("(p j) c -> p j c", j=PACK)[:, :, c0:c1])
             return raw
 
-        def operand(name, cuts, tags={}):
+        def operand(name, cuts, codes_tag=None):
             return [
                 (
                     c0,
                     c1,
-                    keep.tile([P, c1 - c0], U32, name="%s_codes%d" % (name, c0), tag=tags.get(c0, "%s_codes%d" % (name, c0)), align_bytes=64),
+                    keep.tile(
+                        [P, c1 - c0],
+                        U32,
+                        name="%s_codes%d" % (name, c0),
+                        tag=codes_tag or "%s_codes%d" % (name, c0),
+                        align_bytes=64,
+                    ),
                     keep.tile([P, c1 - c0], U8, name="%s_scales%d" % (name, c0), align_bytes=64),
                 )
                 for c0, c1 in zip(cuts, cuts[1:])
             ]
 
         def columns(op, c0, c1):
-            first, last, codes, scales = [piece for piece in op if piece[0] <= c0 and c1 <= piece[1]][0]
+            first, end, codes, scales = [stretch for stretch in op if stretch[0] <= c0 and c1 <= stretch[1]][0]
             return codes[:, c0 - first : c1 - first].bitcast(FP8X4), scales[:, c0 - first : c1 - first]
 
-        def interleave(copy, name, raw, c0, c1, tag=None):
-            grouped = keep.tile([P, c1 - c0, PACK], BF16, name=name + "_grouped", tag=tag or name, align_bytes=64)
+        def interleave(copy, name, raw, c0, c1):
+            staged = keep.tile([P, c1 - c0, PACK], BF16, name=name + "_grouped", tag=name, align_bytes=64)
             copy(
-                out=grouped[:].rearrange("p (c i) j -> p c j i", i=4),
-                in_=raw[:, :, c0:c1].rearrange("p j (c i) -> p c j i", i=4),
+                out=staged[:].rearrange("p (c i) j -> p c j i", i=LINE),
+                in_=raw[:, :, c0:c1].rearrange("p j (c i) -> p c j i", i=LINE),
             )
-            return grouped[:]
+            return staged[:]
 
-        def quantize(op, c0, grouped):
-            codes, scales = columns(op, c0, c0 + grouped.shape[1])
-            nc.vector.quantize_mx(out=codes, scales=scales, in_=grouped.rearrange("p c j -> p (c j)"))
+        def interleave_halves(name, raw, copies):
+            return [interleave(copy, "%s_%d" % (name, i), raw, i * P, (i + 1) * P) for i, copy in enumerate(copies)]
 
-        def mx(acc, w, m, op, c0, c1, start, stop):
-            w_codes, w_scales = columns(w, m * P, (m + 1) * P)
+        def interleave_shared(name, raw):
+            staged = keep.tile([P, UNIT, PACK], BF16, name=name + "_grouped", tag=name, align_bytes=64)
+            for copy, c0, c1 in ((on_scalar, 0, SCALAR_SHARE), (on_vector, SCALAR_SHARE, UNIT)):
+                copy(
+                    out=staged[:, c0:c1, :].rearrange("p (c i) j -> p c j i", i=LINE),
+                    in_=raw[:, :, c0:c1].rearrange("p j (c i) -> p c j i", i=LINE),
+                )
+            return staged[:]
+
+        def quantize(op, c0, staged):
+            codes, scales = columns(op, c0, c0 + staged.shape[1])
+            nc.vector.quantize_mx(out=codes, scales=scales, in_=staged.rearrange("p c j -> p (c j)"))
+
+        def quantize_halves(op, c0, halves):
+            for i, staged in enumerate(halves):
+                quantize(op, c0 + i * P, staged)
+
+        def mx(acc, w_op, m, op, c0, c1, start, stop):
+            w_codes, w_scales = columns(w_op, m * P, (m + 1) * P)
             codes, scales = columns(op, c0, c1)
             nc.tensor.matmul_mx(
                 out=acc, lhsT=w_codes, lhsT_scale=w_scales, rhs=codes, rhs_scale=scales, start=start, stop=stop
             )
 
-        out_rows = out.rearrange("(m p) c -> p m c", p=P)
-        s_grouped = [keep.tile([P, HALF, PACK], BF16, name="s_grouped%d" % h, align_bytes=64) for h in range(2)]
-
-        def gathers():
-            for j in range(PACK):
-                nc.vector.tensor_copy(out=s_grouped[0][:, :, j], in_=planes[j][:].indirect(offsets[:, : HALF // 16]))
-                picked = keep.tile([P, HALF], BF16, name="picked%d" % j)
-                nc.scalar.activation(
-                    picked[:], planes[j][:].indirect(offsets[:, HALF // 16 :]), mybir.ActivationFunctionType.Copy
-                )
-                nc.vector.tensor_copy(out=s_grouped[1][:, :, j], in_=picked[:])
-
-
         def bank(name, b):
             return psum.tile([P, 2 * UNIT], F32, name=name, tag="bank%d" % b)
 
+        out_rows = out.rearrange("(m p) c -> p m c", p=P)
+        s_staged = [keep.tile([P, HALF, PACK], BF16, name="s_grouped%d" % h, align_bytes=64) for h in range(2)]
+
         s_op = operand("s", [0, HALF])
-        x_op = operand("x", [0, UNIT, HALF, HALF + UNIT, S])
+        x_op = operand("x", list(range(0, S + 1, UNIT)))
         w1_op = operand("w1", [0, UNIT, UNIT + P, N])
         w2_op = operand("w2", [0, UNIT, N])
 
-        w2a = load("w2a", w2, 0, UNIT)
-        w1a = load("w1a", w1, 0, UNIT)
+        w2_low = load("w2a", w2, 0, UNIT)
+        w1_low = load("w1a", w1, 0, UNIT)
         x_raw = [load("x0", xT, 0, UNIT)]
-        w2b = load("w2b", w2, UNIT, N)
-        w1b = load("w1b", w1, UNIT, N)
-        x_raw = x_raw + [load("x%d" % u, xT, u * UNIT, (u + 1) * UNIT) for u in range(1, 4)]
+        w2_high = load("w2b", w2, UNIT, N)
+        w1_high = load("w1b", w1, UNIT, N)
+        x_raw = x_raw + [load("x%d" % u, xT, u * UNIT, (u + 1) * UNIT) for u in range(1, LAST + 1)]
 
-        def pair_pass(acc, w, op, u, m, opening):
-            part = acc[:, (m % 2) * UNIT : (m % 2 + 1) * UNIT]
-            mx(part, w, m, op, u * UNIT, (u + 1) * UNIT, opening and m % 2 == 0, not opening and m % 2 == 1)
+        def open_pair(u, h):
+            for i in range(2):
+                mx(pairs[u, h][:, i * UNIT : (i + 1) * UNIT], w2_op, 2 * h + i, s_op, u * UNIT, (u + 1) * UNIT, i == 0, False)
 
-        def close_pair(acc, u, h, tag=None, copy=s):
-            if h == 0:
+        def close_pair(u, h, copy, result_tag=None):
+            acc = pairs[u, h]
+            if h == LOW:
                 for i in range(2):
                     for m in range(2):
                         c0 = u * UNIT + i * P
                         part = acc[:, m * UNIT + i * P : m * UNIT + (i + 1) * P]
                         mx(part, w1_op, m, x_op, c0, c0 + P, False, (i, m) == (1, 1))
             else:
-                for m in (2, 3):
-                    pair_pass(acc, w1_op, x_op, u, m, False)
-            result = keep.tile([P, 2, UNIT], F32, name="early%d_%d" % (u, h), tag=tag or "early%d_%d" % (u, h), align_bytes=64)
+                for i in range(2):
+                    mx(acc[:, i * UNIT : (i + 1) * UNIT], w1_op, 2 + i, x_op, u * UNIT, (u + 1) * UNIT, False, i == 1)
+            name = "early%d_%d" % (u, h)
+            result = keep.tile([P, 2, UNIT], F32, name=name, tag=result_tag or name, align_bytes=64)
             copy(out=result[:].rearrange("p m c -> p (m c)"), in_=acc[:])
             nc.sync.dma_start(out=out_rows[:, 2 * h : 2 * h + 2, u * UNIT : (u + 1) * UNIT], in_=result[:])
-            return result
 
-        def open_one(u, m, b):
-            acc = bank("one%d_%d" % (u, m), b)
-            mx(acc[:, :UNIT], w2_op, m, s_op, u * UNIT, (u + 1) * UNIT, True, False)
+        def open_last_block(m, b):
+            acc = bank("one%d_%d" % (LAST, m), b)
+            mx(acc[:, :UNIT], w2_op, m, s_op, LAST * UNIT, S, True, False)
             return acc
 
-        def close_blocks(accs, u, copies):
-            result = keep.tile([P, 2, UNIT], F32, name="late%d" % u)
+        def close_last_blocks(accs, copies):
+            result = keep.tile([P, 2, UNIT], F32, name="late%d" % LAST)
             for i in range(2):
                 for m in range(2):
-                    c0 = u * UNIT + i * P
+                    c0 = LAST * UNIT + i * P
                     mx(accs[m][:, i * P : (i + 1) * P], w1_op, m, x_op, c0, c0 + P, False, i == 1)
             for m in range(2):
                 copies[m](out=result[:, m, :], in_=accs[m][:, :UNIT])
-            nc.sync.dma_start(out=out_rows[:, :2, u * UNIT : (u + 1) * UNIT], in_=result[:])
+            nc.sync.dma_start(out=out_rows[:, :2, LAST * UNIT :], in_=result[:])
 
-        def halves(u, copies):
-            return [interleave(copies[i], "x%d_%d" % (u, i), x_raw[u], i * P, (i + 1) * P) for i in range(2)]
+        for j in range(PACK):
+            nc.vector.tensor_copy(out=s_staged[0][:, :, j], in_=s_slots[j][:].indirect(offsets[:, : HALF // 16]))
+            picked = keep.tile([P, HALF], BF16, name="picked%d" % j)
+            nc.scalar.activation(
+                picked[:], s_slots[j][:].indirect(offsets[:, HALF // 16 :]), mybir.ActivationFunctionType.Copy
+            )
+            nc.vector.tensor_copy(out=s_staged[1][:, :, j], in_=picked[:])
 
-        def quantize_halves(u, grouped):
-            for i in range(2):
-                quantize(x_op, u * UNIT + i * P, grouped[i])
+        w2_low_staged = interleave(on_scalar, "w2a", w2_low, 0, UNIT)
+        w1_low_staged = interleave(on_scalar, "w1a", w1_low, 0, UNIT)
+        quantize(s_op, 0, s_staged[0][:])
+        quantize(w2_op, 0, w2_low_staged)
+        s_op = s_op + operand("s", [HALF, S], "w2a_raw")
+        quantize(s_op, HALF, s_staged[1][:])
 
-        gathers()
-        g_w2a = interleave(s, "w2a", w2a, 0, UNIT)
-        g_w1a = interleave(s, "w1a", w1a, 0, UNIT)
-        quantize(s_op, 0, s_grouped[0][:])
-        quantize(w2_op, 0, g_w2a)
-        s_op = s_op + operand("s", [HALF, S], {HALF: "w2a_raw"})
-        quantize(s_op, HALF, s_grouped[1][:])
-        def open_pair(u, h):
-            for m in (2 * h, 2 * h + 1):
-                pair_pass(pairs[u, h], w2_op, s_op, u, m, True)
+        pairs = {(u, h): bank("pair%d_%d" % (u, h), 2 * u + h) for u in range(LAST) for h in (LOW, HIGH)}
+        for u in range(LAST):
+            open_pair(u, LOW)
+        last_blocks = [open_last_block(m, 2 * LAST + m) for m in range(2)]
 
-        pairs = {(u, h): bank("pair%d_%d" % (u, h), 2 * u + h) for u in range(3) for h in range(2)}
-        def high_half(name, raw):
-            return [interleave(copy, "%s_%d" % (name, i), raw, i * P, (i + 1) * P) for i, copy in enumerate((v, s))]
+        x_halves = interleave_halves("x0", x_raw[0], (on_vector, on_scalar))
+        quantize(w1_op, 0, w1_low_staged)
+        quantize_halves(x_op, 0, x_halves)
+        w2_high_staged = interleave_shared("w2b", w2_high)
+        w1_high_halves = interleave_halves("w1b", w1_high, (on_vector, on_scalar))
+        quantize(w2_op, UNIT, w2_high_staged)
+        close_pair(0, LOW, on_scalar, "w1b_raw")
+        open_pair(0, HIGH)
+        quantize_halves(w1_op, UNIT, w1_high_halves)
 
-        def quantize_high(op, grouped):
-            for i in range(2):
-                quantize(op, UNIT + i * P, grouped[i])
+        x_halves = interleave_halves("x1", x_raw[1], (on_vector, on_vector))
+        close_pair(0, HIGH, on_scalar)
+        for u in range(1, LAST):
+            open_pair(u, HIGH)
+        quantize_halves(x_op, UNIT, x_halves)
 
-        for u in range(3):
-            open_pair(u, 0)
-        last = [open_one(3, m, 6 + m) for m in range(2)]
-        g_x0 = halves(0, [v, s])
-        quantize(w1_op, 0, g_w1a)
-        quantize_halves(0, g_x0)
-        g_w2b = interleave(s, "w2b", w2b, 0, UNIT)
-        g_w1b = high_half("w1b", w1b)
-        quantize(w2_op, UNIT, g_w2b)
-        close_pair(pairs[0, 0], 0, 0, "w1b_raw")
-        open_pair(0, 1)
-        quantize_high(w1_op, g_w1b)
-        g_x1 = halves(1, [v, v])
-        close_pair(pairs[0, 1], 0, 1)
-        for u in (1, 2):
-            open_pair(u, 1)
-        quantize_halves(1, g_x1)
-        g_x2 = halves(2, [v, v])
-        close_pair(pairs[1, 0], 1, 0)
-        close_pair(pairs[1, 1], 1, 1)
-        pairs[3, 1] = bank("pair3_1", 0)
-        open_pair(3, 1)
-        quantize_halves(2, g_x2)
-        g_x3 = halves(3, [v, v])
-        close_pair(pairs[2, 0], 2, 0)
-        close_pair(pairs[2, 1], 2, 1)
-        quantize_halves(3, g_x3)
-        close_blocks(last, 3, [v, s])
-        close_pair(pairs[3, 1], 3, 1, copy=v)
+        x_halves = interleave_halves("x2", x_raw[2], (on_vector, on_vector))
+        close_pair(1, LOW, on_scalar)
+        close_pair(1, HIGH, on_scalar)
+        pairs[LAST, HIGH] = bank("pair3_1", 0)
+        open_pair(LAST, HIGH)
+        quantize_halves(x_op, 2 * UNIT, x_halves)
+
+        x_halves = interleave_halves("x3", x_raw[LAST], (on_vector, on_vector))
+        close_pair(2, LOW, on_scalar)
+        close_pair(2, HIGH, on_scalar)
+        quantize_halves(x_op, LAST * UNIT, x_halves)
+
+        close_last_blocks(last_blocks, (on_vector, on_scalar))
+        close_pair(LAST, HIGH, on_vector)

@@ -17,7 +17,7 @@ PACK = 4
 HALF = S // 2
 UNIT = 256
 LINE = 4
-SCALAR_SHARE = 192
+LARGE_SHARE = 192
 LOW, HIGH = 0, 1
 LAST = S // UNIT - 1
 
@@ -78,14 +78,20 @@ def tile_picked_recall_none_e_kernel(tc, xT, sT, w1, w2, offs, out):
         def interleave_halves(name, raw, copies):
             return [interleave(copy, "%s_%d" % (name, i), raw, i * P, (i + 1) * P) for i, copy in enumerate(copies)]
 
-        def interleave_shared(name, raw):
-            staged = keep.tile([P, UNIT, PACK], BF16, name=name + "_grouped", tag=name, align_bytes=64)
-            for copy, c0, c1 in ((on_scalar, 0, SCALAR_SHARE), (on_vector, SCALAR_SHARE, UNIT)):
+        def interleave_shared(name, raw, first, cut, end, copies):
+            staged = keep.tile([P, end - first, PACK], BF16, name=name + "_grouped", tag=name, align_bytes=64)
+            for copy, c0, c1 in zip(copies, (first, cut), (cut, end)):
                 copy(
-                    out=staged[:, c0:c1, :].rearrange("p (c i) j -> p c j i", i=LINE),
+                    out=staged[:, c0 - first : c1 - first, :].rearrange("p (c i) j -> p c j i", i=LINE),
                     in_=raw[:, :, c0:c1].rearrange("p j (c i) -> p c j i", i=LINE),
                 )
             return staged[:]
+
+        def interleave_helped(name, raw):
+            return [
+                interleave(on_vector, name + "_0", raw, 0, P),
+                interleave_shared(name + "_1", raw, P, LARGE_SHARE, UNIT, (on_vector, on_scalar)),
+            ]
 
         def quantize(op, c0, staged):
             codes, scales = columns(op, c0, c0 + staged.shape[1])
@@ -178,7 +184,7 @@ def tile_picked_recall_none_e_kernel(tc, xT, sT, w1, w2, offs, out):
         x_halves = interleave_halves("x0", x_raw[0], (on_vector, on_scalar))
         quantize(w1_op, 0, w1_low_staged)
         quantize_halves(x_op, 0, x_halves)
-        w2_high_staged = interleave_shared("w2b", w2_high)
+        w2_high_staged = interleave_shared("w2b", w2_high, 0, LARGE_SHARE, UNIT, (on_scalar, on_vector))
         w1_high_halves = interleave_halves("w1b", w1_high, (on_vector, on_scalar))
         quantize(w2_op, UNIT, w2_high_staged)
         close_pair(0, LOW, on_scalar, "w1b_raw")
@@ -191,7 +197,7 @@ def tile_picked_recall_none_e_kernel(tc, xT, sT, w1, w2, offs, out):
             open_pair(u, HIGH)
         quantize_halves(x_op, UNIT, x_halves)
 
-        x_halves = interleave_halves("x2", x_raw[2], (on_vector, on_vector))
+        x_halves = interleave_helped("x2", x_raw[2])
         close_pair(1, LOW, on_scalar)
         close_pair(1, HIGH, on_scalar)
         pairs[LAST, HIGH] = bank("pair3_1", 0)

@@ -17,9 +17,9 @@ PACK = 4
 HALF = S // 2
 UNIT = 256
 LINE = 4
-LARGE_SHARE = 192
-LOW, HIGH = 0, 1
-LAST = S // UNIT - 1
+EARLY = 3 * P
+UNITS = S // UNIT
+LAST = UNITS - 1
 
 
 def tile_picked_recall_none_e_kernel(tc, xT, sT, w1, w2, offs, out):
@@ -46,66 +46,45 @@ def tile_picked_recall_none_e_kernel(tc, xT, sT, w1, w2, offs, out):
             nc.sync.dma_start(out=raw[:], in_=src.rearrange("(p j) c -> p j c", j=PACK)[:, :, c0:c1])
             return raw
 
-        def operand(name, cuts, codes_tag=None):
-            return [
-                (
-                    c0,
-                    c1,
-                    keep.tile(
-                        [P, c1 - c0],
-                        U32,
-                        name="%s_codes%d" % (name, c0),
-                        tag=codes_tag or "%s_codes%d" % (name, c0),
-                        align_bytes=64,
-                    ),
-                    keep.tile([P, c1 - c0], U8, name="%s_scales%d" % (name, c0), align_bytes=64),
-                )
-                for c0, c1 in zip(cuts, cuts[1:])
-            ]
-
-        def columns(op, c0, c1):
-            first, end, codes, scales = [stretch for stretch in op if stretch[0] <= c0 and c1 <= stretch[1]][0]
-            return codes[:, c0 - first : c1 - first].bitcast(FP8X4), scales[:, c0 - first : c1 - first]
-
-        def interleave(copy, name, raw, c0, c1):
-            staged = keep.tile([P, c1 - c0, PACK], BF16, name=name + "_grouped", tag=name, align_bytes=64)
-            copy(
-                out=staged[:].rearrange("p (c i) j -> p c j i", i=LINE),
-                in_=raw[:, :, c0:c1].rearrange("p j (c i) -> p c j i", i=LINE),
-            )
-            return staged[:]
-
-        def interleave_halves(name, raw, copies):
-            return [interleave(copy, "%s_%d" % (name, i), raw, i * P, (i + 1) * P) for i, copy in enumerate(copies)]
-
-        def interleave_shared(name, raw, first, cut, end, copies):
+        def interleave(name, raw, first, shares):
+            end = shares[-1][1]
             staged = keep.tile([P, end - first, PACK], BF16, name=name + "_grouped", tag=name, align_bytes=64)
-            for copy, c0, c1 in zip(copies, (first, cut), (cut, end)):
+            c0 = first
+            for copy, c1 in shares:
                 copy(
                     out=staged[:, c0 - first : c1 - first, :].rearrange("p (c i) j -> p c j i", i=LINE),
                     in_=raw[:, :, c0:c1].rearrange("p j (c i) -> p c j i", i=LINE),
                 )
+                c0 = c1
             return staged[:]
 
-        def interleave_helped(name, raw):
-            return [
-                interleave(on_vector, name + "_0", raw, 0, P),
-                interleave_shared(name + "_1", raw, P, LARGE_SHARE, UNIT, (on_vector, on_scalar)),
-            ]
+        def quantize(name, staged, codes_tag=None):
+            width = staged.shape[1]
+            codes = keep.tile([P, width], U32, name=name + "_codes", tag=codes_tag or name + "_codes", align_bytes=64)
+            scales = keep.tile([P, width], U8, name=name + "_scales", align_bytes=64)
+            nc.vector.quantize_mx(out=codes[:].bitcast(FP8X4), scales=scales[:], in_=staged.rearrange("p c j -> p (c j)"))
+            return codes, scales
 
-        def quantize(op, c0, staged):
-            codes, scales = columns(op, c0, c0 + staged.shape[1])
-            nc.vector.quantize_mx(out=codes, scales=scales, in_=staged.rearrange("p c j -> p (c j)"))
-
-        def quantize_halves(op, c0, halves):
+        def quantize_halves(name, halves):
+            codes = keep.tile([P, UNIT], U32, name=name + "_codes", align_bytes=64)
+            scales = keep.tile([P, UNIT], U8, name=name + "_scales", align_bytes=64)
             for i, staged in enumerate(halves):
-                quantize(op, c0 + i * P, staged)
+                nc.vector.quantize_mx(
+                    out=codes[:, i * P : (i + 1) * P].bitcast(FP8X4),
+                    scales=scales[:, i * P : (i + 1) * P],
+                    in_=staged.rearrange("p c j -> p (c j)"),
+                )
+            return codes, scales
 
-        def mx(acc, w_op, m, op, c0, c1, start, stop):
-            w_codes, w_scales = columns(w_op, m * P, (m + 1) * P)
-            codes, scales = columns(op, c0, c1)
+        def mx(acc, w_op, w0, op, c0, c1, start, stop):
             nc.tensor.matmul_mx(
-                out=acc, lhsT=w_codes, lhsT_scale=w_scales, rhs=codes, rhs_scale=scales, start=start, stop=stop
+                out=acc,
+                lhsT=w_op[0][:, w0 : w0 + P].bitcast(FP8X4),
+                lhsT_scale=w_op[1][:, w0 : w0 + P],
+                rhs=op[0][:, c0:c1].bitcast(FP8X4),
+                rhs_scale=op[1][:, c0:c1],
+                start=start,
+                stop=stop,
             )
 
         def bank(name, b):
@@ -114,52 +93,11 @@ def tile_picked_recall_none_e_kernel(tc, xT, sT, w1, w2, offs, out):
         out_rows = out.rearrange("(m p) c -> p m c", p=P)
         s_staged = [keep.tile([P, HALF, PACK], BF16, name="s_grouped%d" % h, align_bytes=64) for h in range(2)]
 
-        s_op = operand("s", [0, HALF])
-        x_op = operand("x", list(range(0, S + 1, UNIT)))
-        w1_op = operand("w1", [0, UNIT, UNIT + P, N])
-        w2_op = operand("w2", [0, UNIT, N])
-
-        w2_low = load("w2a", w2, 0, UNIT)
-        w1_low = load("w1a", w1, 0, UNIT)
-        x_raw = [load("x0", xT, 0, UNIT)]
-        w2_high = load("w2b", w2, UNIT, N)
-        w1_high = load("w1b", w1, UNIT, N)
-        x_raw = x_raw + [load("x%d" % u, xT, u * UNIT, (u + 1) * UNIT) for u in range(1, LAST + 1)]
-
-        def open_pair(u, h):
-            for i in range(2):
-                mx(pairs[u, h][:, i * UNIT : (i + 1) * UNIT], w2_op, 2 * h + i, s_op, u * UNIT, (u + 1) * UNIT, i == 0, False)
-
-        def close_pair(u, h, copy, result_tag=None):
-            acc = pairs[u, h]
-            if h == LOW:
-                for i in range(2):
-                    for m in range(2):
-                        c0 = u * UNIT + i * P
-                        part = acc[:, m * UNIT + i * P : m * UNIT + (i + 1) * P]
-                        mx(part, w1_op, m, x_op, c0, c0 + P, False, (i, m) == (1, 1))
-            else:
-                for i in range(2):
-                    mx(acc[:, i * UNIT : (i + 1) * UNIT], w1_op, 2 + i, x_op, u * UNIT, (u + 1) * UNIT, False, i == 1)
-            name = "early%d_%d" % (u, h)
-            result = keep.tile([P, 2, UNIT], F32, name=name, tag=result_tag or name, align_bytes=64)
-            copy(out=result[:].rearrange("p m c -> p (m c)"), in_=acc[:])
-            nc.sync.dma_start(out=out_rows[:, 2 * h : 2 * h + 2, u * UNIT : (u + 1) * UNIT], in_=result[:])
-
-        def open_last_block(m, b):
-            acc = bank("one%d_%d" % (LAST, m), b)
-            mx(acc[:, :UNIT], w2_op, m, s_op, LAST * UNIT, S, True, False)
-            return acc
-
-        def close_last_blocks(accs, copies):
-            result = keep.tile([P, 2, UNIT], F32, name="late%d" % LAST)
-            for i in range(2):
-                for m in range(2):
-                    c0 = LAST * UNIT + i * P
-                    mx(accs[m][:, i * P : (i + 1) * P], w1_op, m, x_op, c0, c0 + P, False, i == 1)
-            for m in range(2):
-                copies[m](out=result[:, m, :], in_=accs[m][:, :UNIT])
-            nc.sync.dma_start(out=out_rows[:, :2, LAST * UNIT :], in_=result[:])
+        w2_early = load("w2a", w2, 0, EARLY)
+        w1_early = load("w1a", w1, 0, EARLY)
+        x_raw = [load("x%d" % u, xT, u * UNIT, (u + 1) * UNIT) for u in range(UNITS)]
+        w2_late = load("w2b", w2, EARLY, N)
+        w1_late = load("w1b", w1, EARLY, N)
 
         for j in range(PACK):
             nc.vector.tensor_copy(out=s_staged[0][:, :, j], in_=s_slots[j][:].indirect(offsets[:, : HALF // 16]))
@@ -169,45 +107,107 @@ def tile_picked_recall_none_e_kernel(tc, xT, sT, w1, w2, offs, out):
             )
             nc.vector.tensor_copy(out=s_staged[1][:, :, j], in_=picked[:])
 
-        w2_low_staged = interleave(on_scalar, "w2a", w2_low, 0, UNIT)
-        w1_low_staged = interleave(on_scalar, "w1a", w1_low, 0, UNIT)
-        quantize(s_op, 0, s_staged[0][:])
-        quantize(w2_op, 0, w2_low_staged)
-        s_op = s_op + operand("s", [HALF, S], "w2a_raw")
-        quantize(s_op, HALF, s_staged[1][:])
+        w2_pair_staged = interleave("w2p", w2_early, 0, [(on_scalar, UNIT)])
+        w2_third_staged = interleave("w2t", w2_early, UNIT, [(on_scalar, EARLY)])
+        s_ops = [quantize("s0", s_staged[0][:])]
+        w2_op = quantize("w2p", w2_pair_staged)
+        s_ops = s_ops + [quantize("s1", s_staged[1][:], "w2a_raw")]
+        w2_third_op = quantize("w2t", w2_third_staged)
+        w1_pair_staged = interleave("w1p", w1_early, 0, [(on_scalar, UNIT)])
 
-        pairs = {(u, h): bank("pair%d_%d" % (u, h), 2 * u + h) for u in range(LAST) for h in (LOW, HIGH)}
-        for u in range(LAST):
-            open_pair(u, LOW)
-        last_blocks = [open_last_block(m, 2 * LAST + m) for m in range(2)]
+        def memories(u):
+            return s_ops[u // 2], (u % 2) * UNIT, (u % 2 + 1) * UNIT
 
-        x_halves = interleave_halves("x0", x_raw[0], (on_vector, on_scalar))
-        quantize(w1_op, 0, w1_low_staged)
-        quantize_halves(x_op, 0, x_halves)
-        w2_high_staged = interleave_shared("w2b", w2_high, 0, LARGE_SHARE, UNIT, (on_scalar, on_vector))
-        w1_high_halves = interleave_halves("w1b", w1_high, (on_vector, on_scalar))
-        quantize(w2_op, UNIT, w2_high_staged)
-        close_pair(0, LOW, on_scalar, "w1b_raw")
-        open_pair(0, HIGH)
-        quantize_halves(w1_op, UNIT, w1_high_halves)
+        pairs, thirds, results, x_ops = {}, {}, {}, {}
 
-        x_halves = interleave_halves("x1", x_raw[1], (on_vector, on_vector))
-        close_pair(0, HIGH, on_scalar)
-        for u in range(1, LAST):
-            open_pair(u, HIGH)
-        quantize_halves(x_op, UNIT, x_halves)
+        def open_pair(u):
+            pairs[u] = bank("pair%d" % u, u)
+            for m in range(2):
+                mx(pairs[u][:, m * UNIT : (m + 1) * UNIT], w2_op, m * P, *memories(u), m == 0, False)
 
-        x_halves = interleave_helped("x2", x_raw[2])
-        close_pair(1, LOW, on_scalar)
-        close_pair(1, HIGH, on_scalar)
-        pairs[LAST, HIGH] = bank("pair3_1", 0)
-        open_pair(LAST, HIGH)
-        quantize_halves(x_op, 2 * UNIT, x_halves)
+        def close(u):
+            for i in range(2):
+                for m in range(2):
+                    part = pairs[u][:, m * UNIT + i * P : m * UNIT + (i + 1) * P]
+                    mx(part, w1_op, m * P, x_ops[u], i * P, (i + 1) * P, False, (i, m) == (1, 1))
 
-        x_halves = interleave_halves("x3", x_raw[LAST], (on_vector, on_vector))
-        close_pair(2, LOW, on_scalar)
-        close_pair(2, HIGH, on_scalar)
-        quantize_halves(x_op, LAST * UNIT, x_halves)
+        def third(u):
+            if u == 1:
+                thirds[1] = thirds[0][:, UNIT:]
+            else:
+                thirds[u] = bank("third%d" % u, (4, 4, 5, 0)[u])
+            mx(thirds[u][:, :UNIT], w1_third_op, 0, x_ops[u], 0, UNIT, u != 1, False)
+            mx(thirds[u][:, :UNIT], w2_third_op, 0, *memories(u), False, u != 0)
 
-        close_last_blocks(last_blocks, (on_vector, on_scalar))
-        close_pair(LAST, HIGH, on_vector)
+        def store_pair(u, tag=None):
+            result = keep.tile([P, 2, UNIT], F32, name="result%d" % u, tag=tag or "result%d" % u, align_bytes=64)
+            on_scalar(out=result[:].rearrange("p m c -> p (m c)"), in_=pairs[u][:])
+            nc.sync.dma_start(out=out_rows[:, :2, u * UNIT : (u + 1) * UNIT], in_=result[:])
+            results[u] = result
+
+        def store_third(u, width, copy, tag=None):
+            result = keep.tile([P, width], F32, name="third_result%d" % u, tag=tag or "third_result%d" % u, align_bytes=64)
+            copy(out=result[:], in_=thirds[u][:, :width])
+            nc.sync.dma_start(out=out_rows[:, 2, u * UNIT : u * UNIT + width], in_=result[:])
+            results[u, 2] = result
+
+        def x_halves(u, cut):
+            if cut == P:
+                second = [(on_scalar, UNIT)]
+            elif cut == UNIT:
+                second = [(on_vector, UNIT)]
+            else:
+                second = [(on_vector, cut), (on_scalar, UNIT)]
+            return [interleave("x%d_0" % u, x_raw[u], 0, [(on_vector, P)]), interleave("x%d_1" % u, x_raw[u], P, second)]
+
+        for u in range(UNITS):
+            open_pair(u)
+
+        halves = x_halves(0, P)
+        w1_third_staged = interleave("x0_raw", w1_early, UNIT, [(on_scalar, EARLY)])
+        w1_op = quantize("w1p", w1_pair_staged)
+        x_ops[0] = quantize_halves("x0", halves)
+        close(0)
+
+        halves = x_halves(1, P)
+        w1_third_op = quantize("w1t", w1_third_staged)
+        third(0)
+        x_ops[1] = quantize_halves("x1", halves)
+        close(1)
+        third(1)
+        store_pair(0, "x1_raw")
+
+        halves = x_halves(2, UNIT)
+        x_ops[2] = quantize_halves("x2", halves)
+        close(2)
+        third(2)
+        store_pair(1)
+        store_third(0, 2 * UNIT, on_scalar)
+
+        halves = x_halves(3, UNIT)
+        x_ops[3] = quantize_halves("x3", halves)
+        close(3)
+        third(3)
+        store_pair(2)
+        store_third(2, UNIT, on_scalar)
+
+        w2_late_staged = interleave("x3_0", w2_late, 0, [(on_vector, P)])
+        w1_late_staged = interleave("w1b", w1_late, 0, [(on_vector, P)])
+        w2_late_op = quantize("w2b", w2_late_staged)
+        w1_late_op = quantize("w1b", w1_late_staged)
+        store_pair(3)
+        store_third(3, UNIT, on_vector, "x3_0")
+
+        quarters = [bank("quarter%d" % u, (6, 7, 1, 2)[u]) for u in range(UNITS)]
+        for u in range(2):
+            mx(quarters[u][:, :UNIT], w2_late_op, 0, *memories(u), True, False)
+        for u in range(2):
+            mx(quarters[u][:, :UNIT], w1_late_op, 0, x_ops[u], 0, UNIT, False, True)
+        for u in range(2, UNITS):
+            mx(quarters[u][:, :UNIT], w1_late_op, 0, x_ops[u], 0, UNIT, True, False)
+            mx(quarters[u][:, :UNIT], w2_late_op, 0, *memories(u), False, True)
+        for h in range(2):
+            result = keep.tile([P, HALF], F32, name="late%d" % h, align_bytes=64)
+            on_vector(out=result[:, :UNIT], in_=quarters[2 * h][:, :UNIT])
+            on_scalar(out=result[:, UNIT:], in_=quarters[2 * h + 1][:, :UNIT])
+            nc.sync.dma_start(out=out[EARLY:, h * HALF : (h + 1) * HALF], in_=result[:])

@@ -118,38 +118,54 @@ def tile_picked_recall_none_e_kernel(tc, xT, sT, w1, w2, offs, out):
         def memories(u):
             return s_ops[u // 2], (u % 2) * UNIT, (u % 2 + 1) * UNIT
 
-        pairs, thirds, results, x_ops = {}, {}, {}, {}
+        pairs, thirds, x_ops = {}, {}, {}
+        results = [keep.tile([P, 3 * UNIT], F32, name="result%d" % u, align_bytes=64) for u in range(UNITS)]
 
         def open_pair(u):
-            pairs[u] = bank("pair%d" % u, u)
-            for m in range(2):
-                mx(pairs[u][:, m * UNIT : (m + 1) * UNIT], w2_op, m * P, *memories(u), m == 0, False)
+            s_op, first, end = memories(u)
+            if u < 2:
+                pairs[u] = bank("pair%d" % u, u)
+                for m in range(2):
+                    mx(pairs[u][:, m * UNIT : (m + 1) * UNIT], w2_op, m * P, s_op, first, end, m == 0, False)
+            else:
+                for i in range(2):
+                    pairs[u, i] = bank("pair%d_%d" % (u, i), 2 * u - 2 + i)
+                    for m in range(2):
+                        c0 = first + i * P
+                        mx(pairs[u, i][:, m * P : (m + 1) * P], w2_op, m * P, s_op, c0, c0 + P, m == 0, False)
 
         def close(u):
             for i in range(2):
                 for m in range(2):
-                    part = pairs[u][:, m * UNIT + i * P : m * UNIT + (i + 1) * P]
-                    mx(part, w1_op, m * P, x_ops[u], i * P, (i + 1) * P, False, (i, m) == (1, 1))
+                    if u < 2:
+                        part, stop = pairs[u][:, m * UNIT + i * P : m * UNIT + (i + 1) * P], (i, m) == (1, 1)
+                    else:
+                        part, stop = pairs[u, i][:, m * P : (m + 1) * P], m == 1
+                    mx(part, w1_op, m * P, x_ops[u], i * P, (i + 1) * P, False, stop)
 
         def third(u):
-            if u == 1:
-                thirds[1] = thirds[0][:, UNIT:]
+            thirds[u] = bank("third%d" % u, 6 + u % 2)
+            mx(thirds[u][:, :UNIT], w1_third_op, 0, x_ops[u], 0, UNIT, True, False)
+            mx(thirds[u][:, :UNIT], w2_third_op, 0, *memories(u), False, True)
+
+        def copy_out(u):
+            if u < 2:
+                on_scalar(out=results[u][:, : 2 * UNIT], in_=pairs[u][:])
             else:
-                thirds[u] = bank("third%d" % u, (4, 4, 5, 0)[u])
-            mx(thirds[u][:, :UNIT], w1_third_op, 0, x_ops[u], 0, UNIT, u != 1, False)
-            mx(thirds[u][:, :UNIT], w2_third_op, 0, *memories(u), False, u != 0)
+                rows = results[u][:].rearrange("p (m c) -> p m c", c=UNIT)
+                for i in range(2):
+                    half = pairs[u, i][:, : 2 * P].rearrange("p (m c) -> p m c", c=P)
+                    on_scalar(out=rows[:, :2, i * P : (i + 1) * P], in_=half)
+            if u == LAST:
+                store(u, 0, 2)
+            on_scalar(out=results[u][:, 2 * UNIT :], in_=thirds[u][:, :UNIT])
+            store(u, 2 if u == LAST else 0, 3)
 
-        def store_pair(u, tag=None):
-            result = keep.tile([P, 2, UNIT], F32, name="result%d" % u, tag=tag or "result%d" % u, align_bytes=64)
-            on_scalar(out=result[:].rearrange("p m c -> p (m c)"), in_=pairs[u][:])
-            nc.sync.dma_start(out=out_rows[:, :2, u * UNIT : (u + 1) * UNIT], in_=result[:])
-            results[u] = result
-
-        def store_third(u, width, copy, tag=None):
-            result = keep.tile([P, width], F32, name="third_result%d" % u, tag=tag or "third_result%d" % u, align_bytes=64)
-            copy(out=result[:], in_=thirds[u][:, :width])
-            nc.sync.dma_start(out=out_rows[:, 2, u * UNIT : u * UNIT + width], in_=result[:])
-            results[u, 2] = result
+        def store(u, m0, m1):
+            nc.sync.dma_start(
+                out=out_rows[:, m0:m1, u * UNIT : (u + 1) * UNIT],
+                in_=results[u][:, m0 * UNIT : m1 * UNIT].rearrange("p (m c) -> p m c", c=UNIT),
+            )
 
         def x_halves(u, cut):
             if cut == P:
@@ -163,42 +179,30 @@ def tile_picked_recall_none_e_kernel(tc, xT, sT, w1, w2, offs, out):
         for u in range(UNITS):
             open_pair(u)
 
-        halves = x_halves(0, P)
-        w1_third_staged = interleave("x0_raw", w1_early, UNIT, [(on_scalar, EARLY)])
+        w1_third_staged = interleave("w1t", w1_early, UNIT, [(on_scalar, EARLY)])
+        halves = x_halves(0, UNIT)
         w1_op = quantize("w1p", w1_pair_staged)
         x_ops[0] = quantize_halves("x0", halves)
         close(0)
 
-        halves = x_halves(1, P)
         w1_third_op = quantize("w1t", w1_third_staged)
         third(0)
-        x_ops[1] = quantize_halves("x1", halves)
-        close(1)
-        third(1)
-        store_pair(0, "x1_raw")
+        halves = x_halves(1, P)
+        for u in range(1, UNITS):
+            x_ops[u] = quantize_halves("x%d" % u, halves)
+            close(u)
+            third(u)
+            copy_out(u - 1)
+            if u < LAST:
+                halves = x_halves(u + 1, UNIT)
 
-        halves = x_halves(2, UNIT)
-        x_ops[2] = quantize_halves("x2", halves)
-        close(2)
-        third(2)
-        store_pair(1)
-        store_third(0, 2 * UNIT, on_scalar)
-
-        halves = x_halves(3, UNIT)
-        x_ops[3] = quantize_halves("x3", halves)
-        close(3)
-        third(3)
-        store_pair(2)
-        store_third(2, UNIT, on_scalar)
-
-        w2_late_staged = interleave("x3_0", w2_late, 0, [(on_vector, P)])
+        w2_late_staged = interleave("x3_raw", w2_late, 0, [(on_vector, P)])
         w1_late_staged = interleave("w1b", w1_late, 0, [(on_vector, P)])
         w2_late_op = quantize("w2b", w2_late_staged)
         w1_late_op = quantize("w1b", w1_late_staged)
-        store_pair(3)
-        store_third(3, UNIT, on_vector, "x3_0")
+        copy_out(LAST)
 
-        quarters = [bank("quarter%d" % u, (6, 7, 1, 2)[u]) for u in range(UNITS)]
+        quarters = [bank("quarter%d" % u, u) for u in range(UNITS)]
         for u in range(2):
             mx(quarters[u][:, :UNIT], w2_late_op, 0, *memories(u), True, False)
         for u in range(2):

@@ -119,7 +119,8 @@ def tile_picked_recall_none_e_kernel(tc, xT, sT, w1, w2, offs, out):
             return s_ops[u // 2], (u % 2) * UNIT, (u % 2 + 1) * UNIT
 
         pairs, thirds, x_ops = {}, {}, {}
-        results = [keep.tile([P, 3 * UNIT], F32, name="result%d" % u, align_bytes=64) for u in range(UNITS)]
+        results = [keep.tile([P, 2 * UNIT], F32, name="result%d" % u, align_bytes=64) for u in range(UNITS)]
+        early_thirds = keep.tile([P, 2 * UNIT], F32, name="early_thirds", align_bytes=64)
 
         def open_pair(u):
             s_op, first, end = memories(u)
@@ -156,10 +157,18 @@ def tile_picked_recall_none_e_kernel(tc, xT, sT, w1, w2, offs, out):
                 for i in range(2):
                     half = pairs[u, i][:, : 2 * P].rearrange("p (m c) -> p m c", c=P)
                     on_scalar(out=rows[:, :2, i * P : (i + 1) * P], in_=half)
-            if u == LAST:
-                store(u, 0, 2)
-            on_scalar(out=results[u][:, 2 * UNIT :], in_=thirds[u][:, :UNIT])
-            store(u, 2 if u == LAST else 0, 3)
+            store(u, 0, 2)
+
+        def copy_third(u):
+            if u < 2:
+                on_scalar(out=early_thirds[:, u * UNIT : (u + 1) * UNIT], in_=thirds[u][:, :UNIT])
+                if u == 1:
+                    nc.sync.dma_start(out=out_rows[:, 2, : 2 * UNIT], in_=early_thirds[:])
+            else:
+                tag = "x3_0" if u == 2 else "third_result"
+                result = keep.tile([P, UNIT], F32, name="third_result%d" % u, tag=tag, align_bytes=64)
+                on_scalar(out=result[:], in_=thirds[u][:, :UNIT])
+                nc.sync.dma_start(out=out_rows[:, 2, u * UNIT : (u + 1) * UNIT], in_=result[:])
 
         def store(u, m0, m1):
             nc.sync.dma_start(
@@ -194,13 +203,16 @@ def tile_picked_recall_none_e_kernel(tc, xT, sT, w1, w2, offs, out):
             third(u)
             copy_out(u - 1)
             if u < LAST:
+                copy_third(u - 1)
                 halves = x_halves(u + 1, UNIT)
+        w2_late_staged = interleave("x3_raw", w2_late, 0, [(on_vector, P // 2), (on_scalar, P)])
+        copy_third(LAST - 1)
 
-        w2_late_staged = interleave("x3_raw", w2_late, 0, [(on_vector, P)])
         w1_late_staged = interleave("w1b", w1_late, 0, [(on_vector, P)])
         w2_late_op = quantize("w2b", w2_late_staged)
         w1_late_op = quantize("w1b", w1_late_staged)
         copy_out(LAST)
+        copy_third(LAST)
 
         quarters = [bank("quarter%d" % u, u) for u in range(UNITS)]
         for u in range(2):

@@ -20,6 +20,7 @@ LINE = 4
 EARLY = 3 * P
 UNITS = S // UNIT
 LAST = UNITS - 1
+ALIGN = 256
 
 
 def tile_picked_recall_none_e_kernel(tc, xT, sT, w1, w2, offs, out):
@@ -35,20 +36,20 @@ def tile_picked_recall_none_e_kernel(tc, xT, sT, w1, w2, offs, out):
         s_rows = sT.rearrange("(p j) t -> p j t", j=PACK)
         s_slots = []
         for j in range(PACK):
-            slot = keep.tile([P, T], F32, name="plane%d" % j)
+            slot = keep.tile([P, T], F32, name="plane%d" % j, align_bytes=ALIGN)
             nc.sync.dma_start(out=slot[:], in_=s_rows[:, j, :])
             s_slots.append(slot)
             if j == 0:
                 nc.sync.dma_start(offsets[:], offs)
 
         def load(name, src, c0, c1):
-            raw = keep.tile([P, PACK, c1 - c0], F32, name=name + "_raw", tag=name + "_raw", align_bytes=64)
+            raw = keep.tile([P, PACK, c1 - c0], F32, name=name + "_raw", tag=name + "_raw", align_bytes=ALIGN)
             nc.sync.dma_start(out=raw[:], in_=src.rearrange("(p j) c -> p j c", j=PACK)[:, :, c0:c1])
             return raw
 
         def interleave(name, raw, first, shares):
             end = shares[-1][1]
-            staged = keep.tile([P, end - first, PACK], BF16, name=name + "_grouped", tag=name, align_bytes=64)
+            staged = keep.tile([P, end - first, PACK], BF16, name=name + "_grouped", tag=name, align_bytes=ALIGN)
             c0 = first
             for copy, c1 in shares:
                 copy(
@@ -60,14 +61,14 @@ def tile_picked_recall_none_e_kernel(tc, xT, sT, w1, w2, offs, out):
 
         def quantize(name, staged, codes_tag=None):
             width = staged.shape[1]
-            codes = keep.tile([P, width], U32, name=name + "_codes", tag=codes_tag or name + "_codes", align_bytes=64)
-            scales = keep.tile([P, width], U8, name=name + "_scales", align_bytes=64)
+            codes = keep.tile([P, width], U32, name=name + "_codes", tag=codes_tag or name + "_codes", align_bytes=ALIGN)
+            scales = keep.tile([P, width], U8, name=name + "_scales", align_bytes=ALIGN)
             nc.vector.quantize_mx(out=codes[:].bitcast(FP8X4), scales=scales[:], in_=staged.rearrange("p c j -> p (c j)"))
             return codes, scales
 
         def quantize_halves(name, halves):
-            codes = keep.tile([P, UNIT], U32, name=name + "_codes", align_bytes=64)
-            scales = keep.tile([P, UNIT], U8, name=name + "_scales", align_bytes=64)
+            codes = keep.tile([P, UNIT], U32, name=name + "_codes", align_bytes=ALIGN)
+            scales = keep.tile([P, UNIT], U8, name=name + "_scales", align_bytes=ALIGN)
             for i, staged in enumerate(halves):
                 nc.vector.quantize_mx(
                     out=codes[:, i * P : (i + 1) * P].bitcast(FP8X4),
@@ -91,7 +92,7 @@ def tile_picked_recall_none_e_kernel(tc, xT, sT, w1, w2, offs, out):
             return psum.tile([P, 2 * UNIT], F32, name=name, tag="bank%d" % b)
 
         out_rows = out.rearrange("(m p) c -> p m c", p=P)
-        s_staged = [keep.tile([P, HALF, PACK], BF16, name="s_grouped%d" % h, align_bytes=64) for h in range(2)]
+        s_staged = [keep.tile([P, HALF, PACK], BF16, name="s_grouped%d" % h, align_bytes=ALIGN) for h in range(2)]
 
         w2_early = load("w2a", w2, 0, EARLY)
         w1_early = load("w1a", w1, 0, EARLY)
@@ -119,8 +120,8 @@ def tile_picked_recall_none_e_kernel(tc, xT, sT, w1, w2, offs, out):
             return s_ops[u // 2], (u % 2) * UNIT, (u % 2 + 1) * UNIT
 
         pairs, thirds, x_ops = {}, {}, {}
-        results = [keep.tile([P, 2 * UNIT], F32, name="result%d" % u, align_bytes=64) for u in range(UNITS)]
-        early_thirds = keep.tile([P, 2 * UNIT], F32, name="early_thirds", align_bytes=64)
+        results = [keep.tile([P, 2 * UNIT], F32, name="result%d" % u, align_bytes=ALIGN) for u in range(UNITS)]
+        early_thirds = keep.tile([P, 2 * UNIT], F32, name="early_thirds", align_bytes=ALIGN)
 
         def open_pair(u):
             s_op, first, end = memories(u)
@@ -166,7 +167,7 @@ def tile_picked_recall_none_e_kernel(tc, xT, sT, w1, w2, offs, out):
                     nc.sync.dma_start(out=out_rows[:, 2, : 2 * UNIT], in_=early_thirds[:])
             else:
                 tag = "x3_0" if u == 2 else "third_result"
-                result = keep.tile([P, UNIT], F32, name="third_result%d" % u, tag=tag, align_bytes=64)
+                result = keep.tile([P, UNIT], F32, name="third_result%d" % u, tag=tag, align_bytes=ALIGN)
                 on_scalar(out=result[:], in_=thirds[u][:, :UNIT])
                 nc.sync.dma_start(out=out_rows[:, 2, u * UNIT : (u + 1) * UNIT], in_=result[:])
 
@@ -223,7 +224,7 @@ def tile_picked_recall_none_e_kernel(tc, xT, sT, w1, w2, offs, out):
             mx(quarters[u][:, :UNIT], w1_late_op, 0, x_ops[u], 0, UNIT, True, False)
             mx(quarters[u][:, :UNIT], w2_late_op, 0, *memories(u), False, True)
         for h in range(2):
-            result = keep.tile([P, HALF], F32, name="late%d" % h, align_bytes=64)
+            result = keep.tile([P, HALF], F32, name="late%d" % h, align_bytes=ALIGN)
             on_vector(out=result[:, :UNIT], in_=quarters[2 * h][:, :UNIT])
             on_scalar(out=result[:, UNIT:], in_=quarters[2 * h + 1][:, :UNIT])
             nc.sync.dma_start(out=out[EARLY:, h * HALF : (h + 1) * HALF], in_=result[:])

@@ -102,17 +102,15 @@ def tile_picked_recall_none_e_kernel(tc, xT, sT, w1, w2, offs, out):
 
         for j in range(PACK):
             nc.vector.tensor_copy(out=s_staged[0][:, :, j], in_=s_slots[j][:].indirect(offsets[:, : HALF // 16]))
-            picked = keep.tile([P, HALF], BF16, name="picked%d" % j)
             nc.scalar.activation(
-                picked[:], s_slots[j][:].indirect(offsets[:, HALF // 16 :]), mybir.ActivationFunctionType.Copy
+                s_staged[1][:, :, j], s_slots[j][:].indirect(offsets[:, HALF // 16 :]), mybir.ActivationFunctionType.Copy
             )
-            nc.vector.tensor_copy(out=s_staged[1][:, :, j], in_=picked[:])
 
         w2_pair_staged = interleave("w2p", w2_early, 0, [(on_scalar, UNIT)])
         w2_third_staged = interleave("w2t", w2_early, UNIT, [(on_scalar, EARLY)])
         s_ops = [quantize("s0", s_staged[0][:])]
         w2_op = quantize("w2p", w2_pair_staged)
-        s_ops = s_ops + [quantize("s1", s_staged[1][:], "w2a_raw")]
+        s_ops = s_ops + [quantize("s1", s_staged[1][:])]
         w2_third_op = quantize("w2t", w2_third_staged)
         w1_pair_staged = interleave("w1p", w1_early, 0, [(on_scalar, UNIT)])
 

@@ -21,6 +21,7 @@ EARLY = 3 * P
 UNITS = S // UNIT
 LAST = UNITS - 1
 ALIGN = 256
+AHEAD = 2 * UNIT - 64
 
 
 def tile_picked_recall_none_e_kernel(tc, xT, sT, w1, w2, offs, out):
@@ -42,9 +43,10 @@ def tile_picked_recall_none_e_kernel(tc, xT, sT, w1, w2, offs, out):
             if j == 0:
                 nc.sync.dma_start(offsets[:], offs)
 
-        def load(name, src, c0, c1):
-            raw = keep.tile([P, PACK, c1 - c0], F32, name=name + "_raw", tag=name + "_raw", align_bytes=ALIGN)
-            nc.sync.dma_start(out=raw[:], in_=src.rearrange("(p j) c -> p j c", j=PACK)[:, :, c0:c1])
+        def load(name, src, c0, c1, raw=None):
+            if raw is None:
+                raw = keep.tile([P, PACK, c1 - c0], F32, name=name + "_raw", tag=name + "_raw", align_bytes=ALIGN)[:]
+            nc.sync.dma_start(out=raw, in_=src.rearrange("(p j) c -> p j c", j=PACK)[:, :, c0:c1])
             return raw
 
         def interleave(name, raw, first, shares):
@@ -96,7 +98,9 @@ def tile_picked_recall_none_e_kernel(tc, xT, sT, w1, w2, offs, out):
 
         w2_early = load("w2a", w2, 0, EARLY)
         w1_early = load("w1a", w1, 0, EARLY)
-        x_raw = [load("x%d" % u, xT, u * UNIT, (u + 1) * UNIT) for u in range(UNITS)]
+        shared = keep.tile([P, AHEAD + PACK * UNIT], F32, name="shared", align_bytes=ALIGN)
+        x1_place = shared[:, AHEAD:].rearrange("p (j c) -> p j c", j=PACK)
+        x_raw = [load("x%d" % u, xT, u * UNIT, (u + 1) * UNIT, x1_place if u == 1 else None) for u in range(UNITS)]
         w2_late = load("w2b", w2, EARLY, N)
         w1_late = load("w1b", w1, EARLY, N)
 
@@ -106,11 +110,10 @@ def tile_picked_recall_none_e_kernel(tc, xT, sT, w1, w2, offs, out):
                 s_staged[1][:, :, j], s_slots[j][:].indirect(offsets[:, HALF // 16 :]), mybir.ActivationFunctionType.Copy
             )
 
-        w2_pair_staged = interleave("w2p", w2_early, 0, [(on_scalar, UNIT)])
+        w2_blocks = [interleave("w2_%d" % m, w2_early, m * P, [(on_scalar, (m + 1) * P)]) for m in range(2)]
         w2_third_staged = interleave("w2t", w2_early, UNIT, [(on_scalar, EARLY)])
-        s_ops = [quantize("s0", s_staged[0][:])]
-        w2_op = quantize("w2p", w2_pair_staged)
-        s_ops = s_ops + [quantize("s1", s_staged[1][:])]
+        s_ops = [quantize("s%d" % h, s_staged[h][:]) for h in (1, 0)][::-1]
+        w2_op = quantize_halves("w2p", w2_blocks)
         w2_third_op = quantize("w2t", w2_third_staged)
         w1_pair_staged = interleave("w1p", w1_early, 0, [(on_scalar, UNIT)])
 
@@ -118,21 +121,22 @@ def tile_picked_recall_none_e_kernel(tc, xT, sT, w1, w2, offs, out):
             return s_ops[u // 2], (u % 2) * UNIT, (u % 2 + 1) * UNIT
 
         pairs, thirds, x_ops = {}, {}, {}
-        results = [keep.tile([P, 2 * UNIT], F32, name="result%d" % u, align_bytes=ALIGN) for u in range(UNITS)]
-        early_thirds = keep.tile([P, 2 * UNIT], F32, name="early_thirds", align_bytes=ALIGN)
+        results = [shared[:, : 2 * UNIT]] + [
+            keep.tile([P, 2 * UNIT], F32, name="result%d" % u, align_bytes=ALIGN)[:] for u in range(1, UNITS)
+        ]
 
-        def open_pair(u):
+        def open_pair(u, m):
             s_op, first, end = memories(u)
             if u < 2:
-                pairs[u] = bank("pair%d" % u, u)
-                for m in range(2):
-                    mx(pairs[u][:, m * UNIT : (m + 1) * UNIT], w2_op, m * P, s_op, first, end, m == 0, False)
+                if m == 0:
+                    pairs[u] = bank("pair%d" % u, u)
+                mx(pairs[u][:, m * UNIT : (m + 1) * UNIT], w2_op, m * P, s_op, first, end, m == 0, False)
             else:
                 for i in range(2):
-                    pairs[u, i] = bank("pair%d_%d" % (u, i), 2 * u - 2 + i)
-                    for m in range(2):
-                        c0 = first + i * P
-                        mx(pairs[u, i][:, m * P : (m + 1) * P], w2_op, m * P, s_op, c0, c0 + P, m == 0, False)
+                    if m == 0:
+                        pairs[u, i] = bank("pair%d_%d" % (u, i), 2 * u - 2 + i)
+                    c0 = first + i * P
+                    mx(pairs[u, i][:, m * P : (m + 1) * P], w2_op, m * P, s_op, c0, c0 + P, m == 0, False)
 
         def close(u):
             for i in range(2):
@@ -152,7 +156,7 @@ def tile_picked_recall_none_e_kernel(tc, xT, sT, w1, w2, offs, out):
             if u < 2:
                 on_scalar(out=results[u][:, : 2 * UNIT], in_=pairs[u][:])
             else:
-                rows = results[u][:].rearrange("p (m c) -> p m c", c=UNIT)
+                rows = results[u].rearrange("p (m c) -> p m c", c=UNIT)
                 for i in range(2):
                     half = pairs[u, i][:, : 2 * P].rearrange("p (m c) -> p m c", c=P)
                     on_scalar(out=rows[:, :2, i * P : (i + 1) * P], in_=half)
@@ -160,6 +164,9 @@ def tile_picked_recall_none_e_kernel(tc, xT, sT, w1, w2, offs, out):
 
         def copy_third(u):
             if u < 2:
+                if u == 0:
+                    early.append(keep.tile([P, 2 * UNIT], F32, name="early_thirds", tag="x1_0", align_bytes=ALIGN))
+                early_thirds = early[0]
                 on_scalar(out=early_thirds[:, u * UNIT : (u + 1) * UNIT], in_=thirds[u][:, :UNIT])
                 if u == 1:
                     nc.sync.dma_start(out=out_rows[:, 2, : 2 * UNIT], in_=early_thirds[:])
@@ -184,18 +191,20 @@ def tile_picked_recall_none_e_kernel(tc, xT, sT, w1, w2, offs, out):
                 second = [(on_vector, cut), (on_scalar, UNIT)]
             return [interleave("x%d_0" % u, x_raw[u], 0, [(on_vector, P)]), interleave("x%d_1" % u, x_raw[u], P, second)]
 
-        for u in range(UNITS):
-            open_pair(u)
+        for m in range(2):
+            for u in range(UNITS):
+                open_pair(u, m)
 
-        w1_third_staged = interleave("w1t", w1_early, UNIT, [(on_scalar, EARLY)])
-        halves = x_halves(0, UNIT)
+        w1_third_staged = interleave("w1t", w1_early, UNIT, [(on_vector, EARLY)])
+        halves = x_halves(0, P)
         w1_op = quantize("w1p", w1_pair_staged)
         x_ops[0] = quantize_halves("x0", halves)
         close(0)
 
         w1_third_op = quantize("w1t", w1_third_staged)
         third(0)
-        halves = x_halves(1, P)
+        halves = x_halves(1, UNIT - P // 2)
+        early = []
         for u in range(1, UNITS):
             x_ops[u] = quantize_halves("x%d" % u, halves)
             close(u)

@@ -69,12 +69,13 @@ def tile_picked_recall_none_e_kernel(tc, xT, sT, w1, w2, offs, out):
             return codes, scales
 
         def quantize_halves(name, halves):
-            codes = keep.tile([P, UNIT], U32, name=name + "_codes", align_bytes=ALIGN)
-            scales = keep.tile([P, UNIT], U8, name=name + "_scales", align_bytes=ALIGN)
+            width = halves[0].shape[1]
+            codes = keep.tile([P, 2 * width], U32, name=name + "_codes", align_bytes=ALIGN)
+            scales = keep.tile([P, 2 * width], U8, name=name + "_scales", align_bytes=ALIGN)
             for i, staged in enumerate(halves):
                 nc.vector.quantize_mx(
-                    out=codes[:, i * P : (i + 1) * P].bitcast(FP8X4),
-                    scales=scales[:, i * P : (i + 1) * P],
+                    out=codes[:, i * width : (i + 1) * width].bitcast(FP8X4),
+                    scales=scales[:, i * width : (i + 1) * width],
                     in_=staged.rearrange("p c j -> p (c j)"),
                 )
             return codes, scales
@@ -216,22 +217,40 @@ def tile_picked_recall_none_e_kernel(tc, xT, sT, w1, w2, offs, out):
         w2_late_staged = interleave("x3_raw", w2_late, 0, [(on_vector, P // 2), (on_scalar, P)])
         copy_third(LAST - 1)
 
-        w1_late_staged = interleave("w1b", w1_late, 0, [(on_vector, P)])
+        w1_late_staged = [
+            interleave("w1b%d" % i, w1_late, i * P // 2, [(on_vector, (i + 1) * P // 2)]) for i in range(2)
+        ]
         w2_late_op = quantize("w2b", w2_late_staged)
-        w1_late_op = quantize("w1b", w1_late_staged)
+        w1_late_op = quantize_halves("w1b", w1_late_staged)
         copy_out(LAST)
         copy_third(LAST)
 
-        quarters = [bank("quarter%d" % u, u) for u in range(UNITS)]
-        for u in range(2):
-            mx(quarters[u][:, :UNIT], w2_late_op, 0, *memories(u), True, False)
-        for u in range(2):
-            mx(quarters[u][:, :UNIT], w1_late_op, 0, x_ops[u], 0, UNIT, False, True)
-        for u in range(2, UNITS):
-            mx(quarters[u][:, :UNIT], w1_late_op, 0, x_ops[u], 0, UNIT, True, False)
-            mx(quarters[u][:, :UNIT], w2_late_op, 0, *memories(u), False, True)
+        pieces = [(0, P), (P, 3 * P), (3 * P, HALF)]
+        x_cols = lambda c0, c1: (x_ops[c0 // UNIT], c0 % UNIT, c0 % UNIT + c1 - c0)
+        banks = {}
+
+        def passes(h, i, first_op, start, stop):
+            c0, c1 = pieces[i]
+            if start:
+                banks[h, i] = bank("late%d_%d" % (h, i), (0, 1, 2, 3, 6, 4)[3 * h + i])
+            acc = banks[h, i]
+            if first_op is w2_late_op:
+                mx(acc[:, : c1 - c0], w2_late_op, 0, s_ops[h], c0, c1, start, stop)
+            else:
+                parts = [(a, min(a + P, c1)) for a in range(c0, c1, P)]
+                for n, (a, b) in enumerate(parts):
+                    cols = x_cols(h * HALF + a, h * HALF + b)
+                    mx(acc[:, a - c0 : b - c0], w1_late_op, 0, *cols, start and n == 0, stop and n == len(parts) - 1)
+
+        for i in range(2):
+            passes(0, i, w2_late_op, True, False)
+        for i in range(2):
+            passes(0, i, w1_late_op, False, True)
+        for h, i in [(0, 2), (1, 1), (1, 0), (1, 2)]:
+            passes(h, i, w1_late_op, True, False)
+            passes(h, i, w2_late_op, False, True)
         for h in range(2):
             result = keep.tile([P, HALF], F32, name="late%d" % h, align_bytes=ALIGN)
-            on_vector(out=result[:, :UNIT], in_=quarters[2 * h][:, :UNIT])
-            on_scalar(out=result[:, UNIT:], in_=quarters[2 * h + 1][:, :UNIT])
+            for i, (c0, c1) in enumerate(pieces):
+                (on_vector if i == 1 else on_scalar)(out=result[:, c0:c1], in_=banks[h, i][:, : c1 - c0])
             nc.sync.dma_start(out=out[EARLY:, h * HALF : (h + 1) * HALF], in_=result[:])

from contextlib import ExitStack

import concourse.mybir as mybir

K, T, S, N = 512, 4096, 1024, 512
FLOPS = 2 * 2 * K * S * N

F32 = mybir.dt.float32
BF16 = mybir.dt.bfloat16
U32 = mybir.dt.uint32
U16 = mybir.dt.uint16
U8 = mybir.dt.uint8
FP8X4 = mybir.dt.float8_e4m3fn_x4

P = 128
PACK = 4
HALF = S // 2
UNIT = 256
LINE = 4
EARLY = 3 * P
UNITS = S // UNIT
LAST = UNITS - 1
ALIGN = 256
AHEAD = 2 * UNIT - 64


def tile_picked_recall_none_e_kernel(tc, xT, sT, w1, w2, offs, out):
    nc = tc.nc
    with ExitStack() as ctx:
        lists = ctx.enter_context(tc.tile_pool(name="lists", bufs=1))
        keep = ctx.enter_context(tc.tile_pool(name="keep", bufs=1))
        psum = ctx.enter_context(tc.psum_pool(name="psum", bufs=1))
        on_vector, on_scalar = nc.vector.tensor_copy, nc.scalar.copy

        offsets = lists.tile([P, S // 16], U16, name="offsets")

        s_rows = sT.rearrange("(p j) t -> p j t", j=PACK)
        s_slots = []
        for j in range(PACK):
            slot = keep.tile([P, T], F32, name="plane%d" % j, align_bytes=ALIGN)
            nc.sync.dma_start(out=slot[:], in_=s_rows[:, j, :])
            s_slots.append(slot)
            if j == 0:
                nc.sync.dma_start(offsets[:], offs)

        def load(name, src, c0, c1, raw=None):
            if raw is None:
                raw = keep.tile([P, PACK, c1 - c0], F32, name=name + "_raw", tag=name + "_raw", align_bytes=ALIGN)[:]
            nc.sync.dma_start(out=raw, in_=src.rearrange("(p j) c -> p j c", j=PACK)[:, :, c0:c1])
            return raw

        def interleave(name, raw, first, shares):
            end = shares[-1][1]
            staged = keep.tile([P, end - first, PACK], BF16, name=name + "_grouped", tag=name, align_bytes=ALIGN)
            c0 = first
            for copy, c1 in shares:
                copy(
                    out=staged[:, c0 - first : c1 - first, :].rearrange("p (c i) j -> p c j i", i=LINE),
                    in_=raw[:, :, c0:c1].rearrange("p j (c i) -> p c j i", i=LINE),
                )
                c0 = c1
            return staged[:]

        def quantize(name, staged, codes_tag=None):
            width = staged.shape[1]
            codes = keep.tile([P, width], U32, name=name + "_codes", tag=codes_tag or name + "_codes", align_bytes=ALIGN)
            scales = keep.tile([P, width], U8, name=name + "_scales", align_bytes=ALIGN)
            nc.vector.quantize_mx(out=codes[:].bitcast(FP8X4), scales=scales[:], in_=staged.rearrange("p c j -> p (c j)"))
            return codes, scales

        def quantize_halves(name, halves):
            width = halves[0].shape[1]
            codes = keep.tile([P, 2 * width], U32, name=name + "_codes", align_bytes=ALIGN)
            scales = keep.tile([P, 2 * width], U8, name=name + "_scales", align_bytes=ALIGN)
            for i, staged in enumerate(halves):
                nc.vector.quantize_mx(
                    out=codes[:, i * width : (i + 1) * width].bitcast(FP8X4),
                    scales=scales[:, i * width : (i + 1) * width],
                    in_=staged.rearrange("p c j -> p (c j)"),
                )
            return codes, scales

        def mx(acc, w_op, w0, op, c0, c1, start, stop):
            nc.tensor.matmul_mx(
                out=acc,
                lhsT=w_op[0][:, w0 : w0 + P].bitcast(FP8X4),
                lhsT_scale=w_op[1][:, w0 : w0 + P],
                rhs=op[0][:, c0:c1].bitcast(FP8X4),
                rhs_scale=op[1][:, c0:c1],
                start=start,
                stop=stop,
            )

        def bank(name, b):
            return psum.tile([P, 2 * UNIT], F32, name=name, tag="bank%d" % b)

        out_rows = out.rearrange("(m p) c -> p m c", p=P)
        s_staged = [keep.tile([P, HALF, PACK], BF16, name="s_grouped%d" % h, align_bytes=ALIGN) for h in range(2)]

        w2_early = load("w2a", w2, 0, EARLY)
        w1_early = load("w1a", w1, 0, EARLY)
        shared = keep.tile([P, AHEAD + PACK * UNIT], F32, name="shared", align_bytes=ALIGN)
        x1_place = shared[:, AHEAD:].rearrange("p (j c) -> p j c", j=PACK)
        x_raw = [load("x%d" % u, xT, u * UNIT, (u + 1) * UNIT, x1_place if u == 1 else None) for u in range(UNITS)]
        w2_late = load("w2b", w2, EARLY, N)
        w1_late = load("w1b", w1, EARLY, N)

        for j in range(PACK):
            nc.vector.tensor_copy(out=s_staged[0][:, :, j], in_=s_slots[j][:].indirect(offsets[:, : HALF // 16]))
            nc.scalar.activation(
                s_staged[1][:, :, j], s_slots[j][:].indirect(offsets[:, HALF // 16 :]), mybir.ActivationFunctionType.Copy
            )

        w2_blocks = [interleave("w2_%d" % m, w2_early, m * P, [(on_scalar, (m + 1) * P)]) for m in range(2)]
        w2_third_staged = interleave("w2t", w2_early, UNIT, [(on_scalar, EARLY)])
        s_ops = [quantize("s%d" % h, s_staged[h][:]) for h in (1, 0)][::-1]
        w2_op = quantize_halves("w2p", w2_blocks)
        w2_third_op = quantize("w2t", w2_third_staged)
        w1_pair_staged = interleave("w1p", w1_early, 0, [(on_scalar, UNIT)])

        def memories(u):
            return s_ops[u // 2], (u % 2) * UNIT, (u % 2 + 1) * UNIT

        pairs, thirds, x_ops = {}, {}, {}
        results = [shared[:, : 2 * UNIT]] + [
            keep.tile([P, 2 * UNIT], F32, name="result%d" % u, align_bytes=ALIGN)[:] for u in range(1, UNITS)
        ]

        def open_pair(u, m):
            s_op, first, end = memories(u)
            if u < 2:
                if m == 0:
                    pairs[u] = bank("pair%d" % u, u)
                mx(pairs[u][:, m * UNIT : (m + 1) * UNIT], w2_op, m * P, s_op, first, end, m == 0, False)
            else:
                for i in range(2):
                    if m == 0:
                        pairs[u, i] = bank("pair%d_%d" % (u, i), 2 * u - 2 + i)
                    c0 = first + i * P
                    mx(pairs[u, i][:, m * P : (m + 1) * P], w2_op, m * P, s_op, c0, c0 + P, m == 0, False)

        def close(u):
            for i in range(2):
                for m in range(2):
                    if u < 2:
                        part, stop = pairs[u][:, m * UNIT + i * P : m * UNIT + (i + 1) * P], (i, m) == (1, 1)
                    else:
                        part, stop = pairs[u, i][:, m * P : (m + 1) * P], m == 1
                    mx(part, w1_op, m * P, x_ops[u], i * P, (i + 1) * P, False, stop)

        def third(u):
            thirds[u] = bank("third%d" % u, 6 + u % 2)
            mx(thirds[u][:, :UNIT], w1_third_op, 0, x_ops[u], 0, UNIT, True, False)
            mx(thirds[u][:, :UNIT], w2_third_op, 0, *memories(u), False, True)

        def copy_out(u):
            if u < 2:
                on_scalar(out=results[u][:, : 2 * UNIT], in_=pairs[u][:])
            else:
                rows = results[u].rearrange("p (m c) -> p m c", c=UNIT)
                for i in range(2):
                    half = pairs[u, i][:, : 2 * P].rearrange("p (m c) -> p m c", c=P)
                    on_scalar(out=rows[:, :2, i * P : (i + 1) * P], in_=half)
            store(u, 0, 2)

        def copy_third(u):
            if u < 2:
                if u == 0:
                    early.append(keep.tile([P, 2 * UNIT], F32, name="early_thirds", tag="x1_0", align_bytes=ALIGN))
                early_thirds = early[0]
                on_scalar(out=early_thirds[:, u * UNIT : (u + 1) * UNIT], in_=thirds[u][:, :UNIT])
                if u == 1:
                    nc.sync.dma_start(out=out_rows[:, 2, : 2 * UNIT], in_=early_thirds[:])
            else:
                tag = "x3_0" if u == 2 else "third_result"
                result = keep.tile([P, UNIT], F32, name="third_result%d" % u, tag=tag, align_bytes=ALIGN)
                on_scalar(out=result[:], in_=thirds[u][:, :UNIT])
                nc.sync.dma_start(out=out_rows[:, 2, u * UNIT : (u + 1) * UNIT], in_=result[:])

        def store(u, m0, m1):
            nc.sync.dma_start(
                out=out_rows[:, m0:m1, u * UNIT : (u + 1) * UNIT],
                in_=results[u][:, m0 * UNIT : m1 * UNIT].rearrange("p (m c) -> p m c", c=UNIT),
            )

        def x_halves(u, cut):
            if cut == P:
                second = [(on_scalar, UNIT)]
            elif cut == UNIT:
                second = [(on_vector, UNIT)]
            else:
                second = [(on_vector, cut), (on_scalar, UNIT)]
            return [interleave("x%d_0" % u, x_raw[u], 0, [(on_vector, P)]), interleave("x%d_1" % u, x_raw[u], P, second)]

        for m in range(2):
            for u in range(UNITS):
                open_pair(u, m)

        w1_third_staged = interleave("w1t", w1_early, UNIT, [(on_vector, EARLY)])
        halves = x_halves(0, P)
        w1_op = quantize("w1p", w1_pair_staged)
        x_ops[0] = quantize_halves("x0", halves)
        close(0)

        w1_third_op = quantize("w1t", w1_third_staged)
        third(0)
        halves = x_halves(1, UNIT - P // 2)
        early = []
        for u in range(1, UNITS):
            x_ops[u] = quantize_halves("x%d" % u, halves)
            close(u)
            third(u)
            copy_out(u - 1)
            if u < LAST:
                copy_third(u - 1)
                halves = x_halves(u + 1, UNIT)
        w2_late_staged = interleave("x3_raw", w2_late, 0, [(on_vector, P // 2), (on_scalar, P)])
        copy_third(LAST - 1)

        w1_late_staged = [
            interleave("w1b%d" % i, w1_late, i * P // 2, [(on_vector, (i + 1) * P // 2)]) for i in range(2)
        ]
        w2_late_op = quantize("w2b", w2_late_staged)
        w1_late_op = quantize_halves("w1b", w1_late_staged)
        copy_out(LAST)
        copy_third(LAST)

        pieces = [(0, P), (P, 3 * P), (3 * P, HALF)]
        x_cols = lambda c0, c1: (x_ops[c0 // UNIT], c0 % UNIT, c0 % UNIT + c1 - c0)
        banks = {}

        def passes(h, i, first_op, start, stop):
            c0, c1 = pieces[i]
            if start:
                banks[h, i] = bank("late%d_%d" % (h, i), (0, 1, 2, 3, 6, 4)[3 * h + i])
            acc = banks[h, i]
            if first_op is w2_late_op:
                mx(acc[:, : c1 - c0], w2_late_op, 0, s_ops[h], c0, c1, start, stop)
            else:
                parts = [(a, min(a + P, c1)) for a in range(c0, c1, P)]
                for n, (a, b) in enumerate(parts):
                    cols = x_cols(h * HALF + a, h * HALF + b)
                    mx(acc[:, a - c0 : b - c0], w1_late_op, 0, *cols, start and n == 0, stop and n == len(parts) - 1)

        for i in range(2):
            passes(0, i, w2_late_op, True, False)
        for i in range(2):
            passes(0, i, w1_late_op, False, True)
        for h, i in [(0, 2), (1, 1), (1, 0), (1, 2)]:
            passes(h, i, w1_late_op, True, False)
            passes(h, i, w2_late_op, False, True)
        for h in range(2):
            result = keep.tile([P, HALF], F32, name="late%d" % h, align_bytes=ALIGN)
            for i, (c0, c1) in enumerate(pieces):
                (on_vector if i == 1 else on_scalar)(out=result[:, c0:c1], in_=banks[h, i][:, : c1 - c0])
            nc.sync.dma_start(out=out[EARLY:, h * HALF : (h + 1) * HALF], in_=result[:])
